import numpy as np, ml_dtypes
CORES = [6,15,38,47]
N = 4
BF = ml_dtypes.bfloat16
W, C, S, RO, B = 4096, 256, 4, 3, 16
def parts(rng):
    x = rng.integers(122, 135, (N, 8, 16, W), dtype=np.int16)
    far = rng.random((N, 8, 16, W), dtype=np.float32) < rng.choice(np.array([0.02, 0.06, 0.1]), (N, 8, 16, 1))
    far = far | (rng.random((N, 8, 1, W)) < 0.02)
    x = np.where(far, rng.integers(0, 256, (N, 8, 16, W), dtype=np.int16), x)
    return x, rng.integers(0, W, (N, 8, 16, C)), rng.integers(0, 4096, (N, 8, 16, 1)), rng.integers(-160, 161, (N, 8, RO, S, C))
def pack(x, c, w, sl):
    return {"xt": np.ascontiguousarray(np.reshape(x, (N, 128, W))).astype(np.float32).astype(BF), "ch": np.ascontiguousarray(np.reshape(c, (N, 128, C))).astype(np.int32),
            "wt": np.ascontiguousarray(np.reshape(w, (N, 128, 1))).astype(np.int32), "sl": np.ascontiguousarray(np.reshape(sl, (N, 8, RO * S * C))).astype(np.int32)}
def setup_inputs(rng):
    return pack(*parts(rng))
def setup_inputs_spread(rng):
    x = np.minimum((np.exp2(8 * rng.random((N, 8, 1, W))) * rng.random((N, 8, 16, W), dtype=np.float32)).astype(np.int16), 255)
    x = np.where(rng.random((N, 8, 16, 1)) < 0.4, 255 - x, x)
    c = np.minimum((W * rng.random((N, 8, 16, C)) ** rng.choice(np.array([0.25, 1.0, 3.0]), (N, 8, 1, C))).astype(np.int64), W - 1)
    w = np.minimum(np.exp2(12 * rng.random((N, 8, 16, 1))).astype(np.int64) - 1, 4095)
    return pack(x, c, w, rng.integers(-255, 256, (N, 8, RO, S, C)))
def setup_inputs_ends(rng):
    b = np.zeros((N, 8, 16, W), bool); sh = int(rng.integers(0, 4))
    for r in range(N):
        for g in range(8):
            md = 4 if g == 7 else (g + r + sh) % 4
            if md == 0: b[r, g] = rng.random((1, W)) < 0.042
            elif md == 1: b[r, g] = rng.random((16, W)) < rng.choice(np.array([0.042, 0.5, 0.958]), (16, 1))
            elif md == 2: b[r, g] = rng.random((1, W)) < 0.958
            elif md == 3: b[r, g] = rng.random((16, W)) < 0.042
            else:
                b[r, g] = rng.random((1, W)) < 0.042; b[r, g, 15] = rng.random(W) < 0.042
    b[:, 7, :, 0] = False; b[:, 7, :, W - 1] = True
    c = np.where(rng.random((N, 8, 16, C)) < rng.choice(np.array([0.0, 0.0625, 0.5, 0.5, 0.9375, 1.0]), (N, 8, 1, C)), W - 1, 0)
    c[:, :, :, 0] = 0; c[:, 7, :, C - 2] = W - 1
    k = np.arange(16); nm = np.where(k % 2 == 0, W - 1, 0); nx = (((nm * 16) >> 6) + nm + 613 * k) & (W - 1)
    c[:, 7, :, C - 1] = nm
    last, first = b[N - 1, 7], b[0, 7]
    last[:, nx] = False; last[:15, nx[0]] = True; last[15, nx] = True
    first[:, nx] = False; first[:, nx[0]] = True
    w = 4095 * rng.integers(0, 2, (N, 8, 16, 1)); w[:, 1, 0] = 0; w[:, 1, 1] = 4095; w[0, 0] = 0; w[N - 1, 7] = 4095
    sl = 510 * rng.integers(0, 2, (N, 8, RO, S, C)) - 255; sl[N - 1, 7, 0, 0, C - 1] = -255
    return pack(255 * b.astype(np.int16), c, w, sl)
def setup_inputs_corners(rng):
    x, c, w, sl = parts(rng); i = np.arange(C)
    x[1, 0] = 255 * rng.integers(0, 2, (16, W))
    pin = 5 * C + int(rng.integers(0, C)) if W == 4096 else -1
    for a, m in ((0, int(rng.choice(np.array([31, 32, 33, 8 * C - 1])))), (2, 8 * C)):
        x[a] = rng.integers(0, 256, (8, 16, 1)); x[a, 7, 15] = 255; x[a, 7, 14] = 0
        ways = np.stack([np.zeros((8, C), np.int64), np.full((8, C), W - 1), np.tile(B * i, (8, 1)), np.tile(B * i + B - 1, (8, 1)), rng.integers(0, W, (8, C))])
        c[a] = np.take_along_axis(ways, rng.integers(0, 5, (1, 8, C)), 0).reshape(8, 1, C)
        o = rng.permutation(8 * C)
        if a == 0: o = o[o != pin]
        h = np.zeros(8 * C, bool); h[o[:m]] = True
        sl[a, :, 0] = -255; sl[a, :, 0, 0] = np.where(h.reshape(8, C), 0, -255)
    if N > 4: x[4, :4] = rng.integers(0, 256, (4, 16, 1))
    c[1, 5] = 0; c[1, 6] = W - 1
    for a in (1, 3):
        sl[a] = rng.choice(np.array([-255, -1, 0, 1, 255]), (8, RO, S, C))
        c[a, :5] = np.where(rng.random((5, 1, C)) < 0.5, B * i + (B - 1) * rng.integers(0, 2, (5, 16, C)), c[a, :5])
    w[:, 1] = 0; w[:, 2] = 4095; w[:, 3, :15] = 0; w[:, 3, 15] = 4095; w[:, 4] = 1
    for g, low in ((0, 0), (6, 4095)):
        v = rng.integers(220, 256, 16); v[14] = 2; v[15] = 1
        z = rng.integers(3500, 4096, 16); z[14] = rng.integers(0, 2048); z[15] = 0
        z[15] = (low - int(np.sum(v * z))) & 4095
        if (int(np.sum(v * z)) >> 12) & 1 == 0: z[14] += 2048
        x[0, g] = v.reshape(16, 1); w[0, g] = z.reshape(16, 1)
    if pin >= 0:
        p = int(rng.integers(0, 16)); x[0, 5, p] = 1; w[0, 5] = 0; w[0, 5, p] = 4075
        first = (((c[0, 5] * 4075) >> 6) + c[0, 5]) & (W - 1)
        c[0, 5] = np.where(first == 2557, 0, c[0, 5]); c[0, 5, :, pin - 5 * C] = 4093; sl[0, 5, 0, 0, pin - 5 * C] = 0
        nx = (2557 + 613 * np.arange(16)) & (W - 1); own = x[1, 5]; own[:, nx] = rng.integers(122, 135, (16, 1))
    return pack(x, c, w, sl)
def setup_inputs_ties(rng):
    x = rng.integers(0, 254, (N, 8, 16, 1), dtype=np.int16) + 2 * (rng.random((N, 8, 16, W), dtype=np.float32) < rng.choice(np.array([0.02, 0.05]), (N, 8, 16, 1))).astype(np.int16)
    c = rng.integers(0, W, (N, 8, 16, C)); few = np.take_along_axis(c, rng.integers(0, 4, (N, 8, 16, C)), 2)
    c = np.where(rng.random((N, 8, 1, C)) < 0.5, few, c); sl = rng.integers(-3, 4, (N, 8, RO, S, C))
    x[0] = rng.integers(0, 256, (8, 16, 1)); x[2, :2] = rng.integers(0, 256, (2, 16, 1)); c[0] = rng.integers(0, W, (8, 1, C))
    x[1, :, 15] = rng.integers(0, 254, (8, 1)) + 2 * (np.arange(W) & 1)
    h = np.zeros(8 * C, bool); h[rng.permutation(8 * C)[:26 + 2 * int(rng.integers(0, 3)) + 32 * int(rng.integers(0, C // 4))]] = True
    sl[0, :, 0] = -1; sl[0, :, 0, 0] = np.where(h.reshape(8, C), 0, -1)
    return pack(x, c, rng.integers(0, 4096, (N, 8, 16, 1)), sl)
def check_inputs(d):
    bad = []
    for k, lo, hi in (("xt", 0, 255), ("ch", 0, W - 1), ("wt", 0, 4095), ("sl", -255, 255)):
        v = np.asarray(d[k]).astype(np.float64)
        if not (np.min(v) >= lo and np.max(v) <= hi): bad.append("range of " + k)
        if not np.all(v == np.floor(v)): bad.append("whole numbers in " + k)
    return bad
def look(tab, c):
    v = np.take_along_axis(tab, c.reshape(8, 1, 16 * C), 2).reshape(8, 16, 16, C)
    y = np.max(v, axis=2).astype(np.int64); m = np.min(v, axis=2).astype(np.int64)
    return y, np.add.reduce(y - m, axis=1)
def reference(xt, ch, wt, sl):
    X = xt.astype(np.float32).astype(np.int32).reshape(N, 8, 16, W); c = ch.astype(np.int64).reshape(N, 8, 16, C)
    w = wt.astype(np.int64).reshape(N, 8, 16, 1); slack = sl.astype(np.int64).reshape(N, 8, RO, S, C)
    kappa = np.zeros(N, np.int64); k613 = (613 * np.arange(16)).reshape(1, 16, 1)
    for t in range(RO):
        states, tops, wrong = [], [], []
        for r in range(N):
            q = (r + 1 + t % (N - 1)) % N
            s = c[r]; y, e = look(X[r], s); eq = look(X[q], s)[1]
            fs, fy = s, y; right = np.ones((8, C), bool)
            for j in range(S):
                u = np.add.reduce(w[r] * y, axis=1) & 4095
                n = (((s * u[:, None, :]) >> 6) + s + k613 + 77 * j + kappa[r]) & (W - 1)
                yn, en = look(X[r], n); qn = look(X[q], n)[1]; a = slack[r, :, t, j]
                guess = en <= e + a; true = en + qn <= e + eq + a
                go = (right & true)[:, None, :]; fs = np.where(go, n, fs); fy = np.where(go, yn, fy)
                right = right & (guess == true)
                on = guess[:, None, :]; s = np.where(on, n, s); y = np.where(on, yn, y); e = np.where(guess, en, e); eq = np.where(guess, qn, eq)
            states.append(fs); tops.append(fy); wrong.append(np.count_nonzero(~right) & 31)
        for r in range(N):
            place = (B * np.arange(C)[None, :] + (np.add.reduce(w[r] * tops[r], axis=1) & (B - 1)))[:, None, :]
            old = np.take_along_axis(X[r], place, 2)
            np.put_along_axis(X[r], place, ((old + tops[r]) >> 1).astype(np.int32), 2)
        c = np.stack(states); kappa = np.array(wrong, np.int64)
    return {"yc": c.reshape(N, 128, C).astype(np.float32), "yx": X.reshape(N, 128, W).astype(np.float32).astype(BF)}

@@ -1,0 +1,521 @@
+from concourse.mybir import AluOpType, AxisListType, ActivationFunctionType
+
+RO = 3
+SEG = 2048
+NG = 6
+
+SCRATCH = {}
+for _names, _d in (
+        ("tab:4096 gat:12288 ymax:20480 ymin:4096 cmax:4096 mkx:2048 mkn:2048 idb:128 oneb:128 rb1:16 rb2:16 rb3:16 r8:256 "
+         "diag:256 slb:256 per:96 cd:16 wr:16 rc:128 cm:256 lsc:256 fy:256", "bfloat16"),
+        ("nm:1280 nc:256 qt:256 uarr:64 u0:16 um:16 ki:8 tmi:256 ian:16 iav:16 wti:1 wia:4 sli:256 lowa:64 low0:16 low4:16 "
+         "ci:16 ca:16 off:16 lo:16 vi:16 sm:256 sh:256", "int32"),
+        ("lst:3840 clst:3840 nl:16 yl:16 vu:16", "uint16"),
+        ("eret:240 eqin:240 pt:256 es:16 hd:16 darr:64 h1:64 h3:16 tt:240 row:256 lu:128 lp:128 sp:512 sx:256 k613:128 k77:8 "
+         "kl:8 kc:4 one:128 idf:128 bo:8 mk:64 c16:64 wf:4 a4:192 nh:64 he:64 esq:64 dq:64 dtt:64 dd:64 ne:80 wre:64 go:64 "
+         "cod:64 cod4:16 gco:64 sco:64 cp:16 th0:16 thr:16 nw:16 c4m:16 d3:16 gcx:16 ne3:16 ycf:256", "float32")):
+    for _n in _names.split():
+        SCRATCH[_n.split(":")[0]] = ("sbuf", [128, int(_n.split(":")[1])], _d)
+for _b in range(8):
+    SCRATCH["ps%d" % _b] = ("psum", [128, 512], "float32")
+
+SEMAPHORES = ["v_q", "s_q", "p_q", "g_q", "snt", "ldc", "ldx", "ldw", "ldl", "stc", "stx0", "stx1"]
+for _t in range(RO):
+    SEMAPHORES += ["r%d_0" % _t, "e1_%d" % _t, "e2_%d" % _t]
+    for _l in range(1, 5):
+        SEMAPHORES += ["r%d_%d_%d" % (_t, _l, _h) for _h in range(2)]
+
+
+def rank_program(g, core, T, topo):
+    rank = T.rank_of(core)
+    if rank is None:
+        return
+    n_ranks = len(T.cores)
+    A, COPY = AluOpType, ActivationFunctionType.Copy
+    eng = {"v": g.vector, "s": g.scalar, "p": g.tensor, "g": g, "y": g.sync}
+    know = {q: {} for q in eng}
+    snap = {}
+    total = {}
+    wrote, red = {}, {}
+
+    def need(q, s, c):
+        if know[q].get(s, 0) >= c:
+            return
+        eng[q].wait_ge(T.sem[s], c)
+        know[q][s] = c
+        for s2, c2 in snap.get((s, c), {}).items():
+            know[q][s2] = max(know[q].get(s2, 0), c2)
+
+    def pre(q, reads, writes):
+        want = {}
+        for k in list(reads) + list(writes):
+            if k in wrote and not (q == "p" and wrote[k][0] == "p_q"):
+                s, c = wrote[k]
+                want[s] = max(want.get(s, 0), c)
+        for k in writes:
+            for s, c in red.get(k, {}).items():
+                want[s] = max(want.get(s, 0), c)
+        order = sorted(want, key=lambda s: (s == q + "_q", s))
+        full = {s: snap.get((s, want[s]), {}) for s in order}
+        for s in order:
+            if not any(full[o].get(s, 0) >= want[s] and full[s].get(o, 0) < want[o] for o in order if o != s):
+                need(q, s, want[s])
+        for s in order:
+            need(q, s, want[s])
+
+    def run(q, reads, writes, fn, sem=None, inc=1):
+        pre(q, reads, writes)
+        s = sem or q + "_q"
+        c = total[s] = total.get(s, 0) + inc
+        fn(eng[q]).then_inc(T.sem[s], inc)
+        snap[(s, c)] = dict(know[q])
+        snap[(s, c)][s] = c
+        for k in reads:
+            red.setdefault(k, {})[s] = c
+        for k in writes:
+            wrote[k] = (s, c)
+            red[k] = {}
+
+    def V(reads, writes, fn):
+        run("v", reads, writes, fn)
+
+    def tcopy(out, in_, reads, writes):
+        V(reads, writes, lambda e: e.tensor_copy(out, in_))
+
+    def ttens(out, a, b, op, reads, writes):
+        V(reads, writes, lambda e: e.tensor_tensor(out, a, b, op))
+
+    def tsc(out, a, s1, op0, reads, writes, s2=None, op1=None):
+        if op1 is None:
+            V(reads, writes, lambda e: e.tensor_scalar(out, a, s1, None, op0))
+        else:
+            V(reads, writes, lambda e: e.tensor_scalar(out, a, s1, s2, op0, op1))
+
+    def scan(out, d0, d1, init, o0, o1, reads, writes):
+        V(reads, writes, lambda e: e.tensor_tensor_scan(out, d0, d1, init, o0, o1))
+
+    def fill(ap, x, writes):
+        V([], writes, lambda e: e.memset(ap, x))
+
+    def mm(out, lhsT, rhs, start, stop, reads, writes):
+        run("p", reads, writes, lambda e: e.matmul(out, lhsT, rhs, start, stop))
+
+    def sel(out, in_, pattern, op, fillv, base, cm, reads, writes):
+        run("g", reads, writes, lambda e: e.affine_select(out, in_, pattern, op, fillv, base, cm))
+
+    def num(ap, pattern, base, cm, key):
+        run("g", [], [key], lambda e: e.iota(ap, pattern, base, cm, allow_small_or_imprecise_dtypes=True))
+
+    def send(dst, out, in_, rsem, reads):
+        pre("g", reads, [])
+        rid, pid, _ = topo.addr(dst)
+        g.remote_dma(out, in_, T.sem[rsem], T.sem["snt"], pid, rid, topo.mask(core, dst))
+        total["snt"] = total.get("snt", 0) + len(topo.engines(core, dst))
+
+    def arrives(key, s, src):
+        c = total[s] = len(topo.engines(src, core))
+        wrote[key] = (s, c)
+
+    run("y", [], [("nm", 0, 0), ("nm", 0, 1)], lambda e: e.dma_start(T.nm[:, 0:256], T.ch[:, :]), "ldc", 16)
+    run("s", [], ["tab"], lambda e: e.dma_start(T.tab[:, :], T.xt[:, :]), "ldx", 16)
+    run("y", [], ["wti"], lambda e: e.dma_start(T.wti[:, :], T.wt[:, :]), "ldw", 16)
+    for i in range(2):
+        g.sync.dma_start(T.sli[0:96, i * 128:(i + 1) * 128], T.sl[4 * i:4 * i + 4, :]).then_inc(T.sem["ldl"], 16)
+    total["ldl"] = 32
+    wrote["sli"] = ("ldl", 32)
+
+    def lists(t, l, h=None):
+        a = (t * 5 + l) * 256
+        return slice(a, a + 256) if h is None else slice(a + h * 128, a + h * 128 + 128)
+
+    partner = [T.cores[(rank + 1 + t % (n_ranks - 1)) % n_ranks] for t in range(RO)]
+    client = [T.cores[(rank - 1 - t % (n_ranks - 1)) % n_ranks] for t in range(RO)]
+    for t in range(RO):
+        arrives(("cl", t, 0), "r%d_0" % t, client[t])
+        for l in range(1, 5):
+            for h in range(2):
+                arrives(("cl", t, l, h), "r%d_%d_%d" % (t, l, h), client[t])
+        arrives(("e1", t), "e1_%d" % t, partner[t])
+        arrives(("e2", t), "e2_%d" % t, partner[t])
+
+    def send_start(t):
+        send(partner[t], T.clst[:, lists(t, 0)], T.lst[:, lists(t, 0)], "r%d_0" % t, [("L", t, 0, 0), ("L", t, 0, 1)])
+
+    fill(T.one[:, :], 1.0, ["one"])
+    tcopy(T.lst[:, lists(0, 0)], T.nm[:, 0:256], [("nm", 0, 0), ("nm", 0, 1)], [("L", 0, 0, 0), ("L", 0, 0, 1)])
+    fill(T.mkx[:, :], 255.0, ["mkx"])
+    fill(T.mkx[:, ::16], 0.0, ["mkx"])
+    fill(T.mkn[:, :], 0.0, ["mkn"])
+    fill(T.mkn[:, ::16], 255.0, ["mkn"])
+    fill(T.oneb[:, :], 1.0, ["oneb"])
+    fill(T.row[:, :], 1.0, [("row", 0), ("row", 1)])
+    fill(T.kc[:, :], 0.0, ["kc"])
+    fill(T.mk[:, :], 1.0, ["mk"])
+    fill(T.mk[:, ::4], 0.0, ["mk"])
+    fill(T.h1[:, ::4], 1.0, [("h1", 0)])
+    fill(T.ne[:, 0:16], 0.0, ["ne0"])
+    fill(T.darr[:, :], 0.0, ["D"])
+    fill(T.uarr[:, :], 0, ["U"])
+    fill(T.rb2[:, 0:8], 0.0, ["rb2"])
+    fill(T.rb3[:, 8:16], 0.0, ["rb3b"])
+    sel(T.bo[:, :], T.one[:, 0:8], [[-16, 8]], A.is_ge, 0.0, 0, 1, ["one"], ["bo"])
+    sel(T.bo[:, :], T.bo[:, :], [[16, 8]], A.is_ge, 0.0, 15, -1, ["bo"], ["bo"])
+    num(T.k77[:, 0:4], [[77, 4]], -77, 0, "k77")
+    sel(T.idf[:, :], T.one[:, :], [[-1, 128]], A.is_equal, 0.0, 0, 1, ["one"], ["idf"])
+
+    def spread(m, src, r0):
+        o = T.sp[0:25, m * 128:m * 128 + 128]
+        sel(o, src[0:25, :], [[1, 128]], A.is_ge, 0.0, 16 * r0, -16, ["one", "k613"], [("sp", m)])
+        sel(o, o, [[-1, 128]], A.is_ge, 0.0, 15 - 16 * r0, 16, [("sp", m)], [("sp", m)])
+
+    spread(0, T.one, 0)
+    send_start(0)
+    sel(T.lu[0:25, :], T.sp[0:25, 0:128], [[0, 128]], A.is_gt, 64.0, 24, -1, [("sp", 0)], ["lu"])
+    num(T.k613[0:25, :], [[0, 8], [613, 16]], 0, 0, "k613")
+    spread(2, T.one, 16)
+    spread(3, T.k613, 8)
+
+    def kappa_rows():
+        tsc(T.kl[:, 0:4], T.k77[:, 0:4], T.kc[:, 0:1], A.add, ["k77", "kc"], ["kl"])
+
+    def constants_b():
+        tsc(T.wia[:, 0:1], T.wti[:, :], 0xF00, A.bitwise_and, ["wti"], ["wia"])
+        tsc(T.wia[:, 1:2], T.wti[:, :], 255, A.bitwise_and, ["wti"], ["wib"])
+        tcopy(T.rb1[:, 0:8], T.bo[:, :], ["bo"], ["rb1"])
+        tcopy(T.wf[:, 0:2], T.wia[:, 0:2], ["wia", "wib"], ["wf"])
+        tsc(T.rb3[:, 0:8], T.bo[:, :], -1.0, A.mult, ["bo"], ["rb3"])
+        tsc(T.rb1[:, 8:16], T.bo[:, :], T.wf[:, 0:1], A.mult, ["bo", "wf"], ["rb1b"])
+        tsc(T.rb2[:, 8:16], T.bo[:, :], T.wf[:, 1:2], A.mult, ["bo", "wf"], ["rb2b"])
+        kappa_rows()
+        tsc(T.lp[0:25, :], T.sp[0:25, 0:128], 2048.0, A.mult, [("sp", 0)], ["lp"])
+        for m in (2, 3):
+            o = T.sx[0:25, (m - 2) * 128:(m - 1) * 128]
+            tsc(o, T.sp[0:25, m * 128:m * 128 + 128], 64.0, A.mult, [("sp", m)], [("sx", m)])
+            ttens(T.lp[0:25, :], T.lp[0:25, :], o, A.add, [("sx", m), "lp"], ["lp"])
+        sel(T.lp[0:25, :], T.lp[0:25, :], [[0, 128]], A.is_gt, float(2048 * 64 + 64 * 77 - (1 << 23)), 24, -1, ["lp"], ["lp"])
+        for h in range(2):
+            sel(T.per[0:96, h * 48:h * 48 + 48], T.oneb[0:96, 0:48], [[8, 3], [24, 4], [2, 4]], A.is_equal, 0.0, h, -1,
+                ["oneb"], [("per", h)])
+        num(T.c16[:, :], [[0, 16], [16, 4]], 16, 0, "c16")
+        num(T.ian[:, :], [[0, 16]], 0, 1, "ian")
+        num(T.iav[:, :], [[16, 16]], 0, 0, "iav")
+        num(T.tmi[:, :], [[-1, 256]], 4096, 1, "tmi")
+        spread(1, T.one, 8)
+
+    def constants_c():
+        tcopy(T.slb[0:96, :], T.sli[0:96, :], ["sli"], ["slb"])
+        for t in range(RO):
+            for h in range(2):
+                for i in range(2):
+                    o = t * 64 + h * 32 + i * 16
+                    mm(T.ps7[:, o:o + 16], T.slb[0:96, i * 128:i * 128 + 128], T.per[0:96, h * 48 + t * 16:h * 48 + t * 16 + 16],
+                       True, True, ["slb", ("per", h)], ["ps7"])
+        tcopy(T.idb[:, :], T.idf[:, :], ["idf"], ["idb"])
+        tsc(T.tmi[:, :], T.tmi[:, :], 15, A.bitwise_and, ["tmi"], ["tmi"])
+        tsc(T.ian[:, :], T.ian[:, :], 15, A.bitwise_and, ["ian"], ["ian"])
+        tsc(T.diag[:, :], T.tmi[:, :], 0.0, A.is_equal, ["tmi"], ["diag"])
+        ttens(T.ian[:, :], T.ian[:, :], T.iav[:, :], A.add, ["ian", "iav"], ["ian"])
+        for h in range(2):
+            tcopy(T.r8[0:16, h * 128:h * 128 + 128], T.sp[0:16, h * 128:h * 128 + 128], [("sp", h)], [("r8", h)])
+        tsc(T.iav[:, :], T.ian[:, :], 16.0, A.mult, ["ian"], ["iav"])
+        tcopy(T.a4[:, :], T.ps7[:, 0:192], ["ps7"], ["a4"])
+
+    def start_names(t):
+        both = [("L", t, 0, 0), ("L", t, 0, 1)]
+        if t:
+            tcopy(T.nm[:, 0:256], T.lst[:, lists(t, 0)], both, [("nm", 0, 0), ("nm", 0, 1)])
+        tsc(T.nc[:, :], T.lst[:, lists(t, 0)], -2048.0, A.add, both, [("nc", 0), ("nc", 1)])
+
+    slot, mslot, where = [0], [0], {}
+
+    def gather(q, key, src, a, reads, part):
+        if key not in where:
+            slot[0] = (slot[0] + 1) % NG
+            where[key] = slot[0]
+        s = where[key]
+        p0, p1 = (0, 2) if part is None else (part, part + 1)
+        out = T.gat[:, s * SEG + p0 * SEG // 2:s * SEG + p1 * SEG // 2]
+        win = T.tab[:, :].indirect(src[:, a + p0 * 64:a + p1 * 64])
+        keys = [("g", s, p) for p in range(p0, p1)]
+        if q == "s":
+            run("s", reads + ["tab"], keys, lambda e: e.activation(out, win, COPY))
+        else:
+            V(reads + ["tab"], keys, lambda e: e.tensor_copy(out, win))
+
+    def gather_own(q, t, l, h, part=None):
+        gather(q, ("o", t, l, h), T.lst, (t * 5 + l) * 256 + h * 128, [("L", t, l, h)], part)
+
+    def gather_client(q, t, l, h, part=None):
+        gather(q, ("c", t, l, h), T.clst, (t * 5 + l) * 256 + h * 128, [("cl", t, 0) if l == 0 else ("cl", t, l, h)], part)
+
+    def scan_max(key):
+        s = where[key]
+        kind, t, l, h = key
+        out, kk = (T.ymax[:, l * 4096 + h * SEG:l * 4096 + (h + 1) * SEG], ("y", l, h)) if kind == "o" else \
+            (T.cmax[:, h * SEG:(h + 1) * SEG], ("cy", h))
+        scan(out, T.mkx[:, :], T.gat[:, s * SEG:(s + 1) * SEG], 0.0, A.min, A.max, ["mkx", ("g", s, 0), ("g", s, 1)], [kk])
+
+    def scan_min(key):
+        s = where[key]
+        kind, t, l, h = key
+        m = mslot[0] = mslot[0] ^ 1
+        scan(T.ymin[:, m * SEG:(m + 1) * SEG], T.mkn[:, :], T.gat[:, s * SEG:(s + 1) * SEG], 255.0, A.max, A.min,
+             ["mkn", ("g", s, 0), ("g", s, 1)], [("m", m)])
+        mn = T.ymin[:, m * SEG + 15:(m + 1) * SEG:16]
+        if kind == "o":
+            b = "ps%d" % h
+            y0 = l * 4096 + h * SEG
+            y = T.ymax[:, y0 + 15:y0 + SEG:16]
+            out = T[b][:, 0:16]
+            mm(out, y, T.rb1[:, :], True, False, ["rb1", "rb1b", ("y", l, h)], [b])
+            mm(out, y, T.rb2[:, :], False, False, ["rb2", "rb2b", ("y", l, h)], [b])
+            mm(out, mn, T.rb3[:, :], False, True, ["rb3", "rb3b", ("m", m)], [b])
+        else:
+            y = T.cmax[:, h * SEG + 15:(h + 1) * SEG:16]
+            out = T.ps2[:, h * 8:h * 8 + 8]
+            mm(out, y, T.rb1[:, 0:8], True, False, ["rb1", ("cy", h)], ["ps2"])
+            mm(out, mn, T.rb3[:, 0:8], False, True, ["rb3", ("m", m)], ["ps2"])
+
+    def keep_spans(t, l):
+        a = t * 80
+        o = T.eret[:, a + l:a + 64:4] if l < 4 else T.eret[:, a + 64:a + 80]
+        tcopy(o, T.ps2[:, 0:16], ["ps2"], [("er", t, l)])
+        yield
+
+    def return_spans(t, part):
+        a = t * 80 + (64 if part else 0)
+        n = 16 if part else 64
+        ls = [4] if part else range(4)
+        send(client[t], T.eqin[:, a:a + n], T.eret[:, a:a + n], "e%d_%d" % (part + 1, t), [("er", t, l) for l in ls])
+
+    def weave(*parts):
+        live = list(parts)
+        while live:
+            for x in list(live):
+                if next(x, "end") == "end":
+                    live.remove(x)
+
+    def guess(t, l, h):
+        b = "ps%d" % h
+        E, U = T[b][:, 0:8], T[b][:, 8:16]
+        es = T.es[:, h * 8:h * 8 + 8]
+        um = T.um[:, h * 8:h * 8 + 8]
+        o = (l * 2 + h) * 24
+        H = T.tt[:, o + 8:o + 16]
+        j = l - 1
+        if l == 0:
+            u0 = T.u0[:, h * 8:h * 8 + 8]
+            tcopy(u0, U, [b], [("u0", h)])
+            yield
+            fill(H, 1.0, [("th", 0, h)])
+            yield
+            tsc(um, u0, 4095, A.bitwise_and, [("u0", h)], [("um", h)])
+            yield
+            tcopy(es, E, [b], [("es", h)])
+            yield
+            tcopy(T.tt[:, o:o + 8], um, [("um", h)], [("tu", 0, h)])
+            yield
+        else:
+            D = T.darr[:, h * 32 + j:h * 32 + 32:4]
+            Ua = T.uarr[:, h * 32 + j:h * 32 + 32:4]
+            a = T.a4[:, t * 64 + h * 32 + j:t * 64 + h * 32 + 32:4]
+            ttens(D, E, es, A.subtract, [b, ("es", h), "D"], [("D", j, h)])
+            yield
+            tcopy(Ua, U, [b, "U"], [("U", j, h)])
+            yield
+            if l == 4:
+                ttens(T.h3[:, h * 8:h * 8 + 8], D, a, A.is_le, [("D", j, h), "a4"], [("h3", h)])
+                return
+            ttens(H, D, a, A.is_le, [("D", j, h), "a4"], [("th", l, h)])
+            yield
+            tsc(um, Ua, 4095, A.bitwise_and, [("U", j, h)], [("um", h)])
+            yield
+        tsc(T.tt[:, o + 16:o + 24], H, T.kl[:, l:l + 1], A.mult, [("th", l, h), "kl"], [("tk", l, h)])
+        yield
+        if l:
+            ttens(T.tt[:, o:o + 8], um, H, A.mult, [("um", h), ("th", l, h)], [("tu", l, h)])
+        mm(T.ps4[0:24, h * 128:h * 128 + 128], T.tt[:, o:o + 24], T.idf[:, :], True, True,
+           [("tu", l, h), ("th", l, h), ("tk", l, h), "idf"], ["ps4"])
+        yield
+        if l:
+            ttens(T.hd[:, h * 8:h * 8 + 8], H, D, A.mult, [("th", l, h), ("D", j, h)], [("hd", h)])
+            yield
+
+    def rows(l, h):
+        r = T.row[0:25, h * 128:h * 128 + 128]
+        tcopy(T.row[0:24, h * 128:h * 128 + 128], T.ps4[0:24, h * 128:h * 128 + 128], ["ps4"], [("row", h)])
+        mm(T.ps5[:, 0:128], T.lu[0:25, :], r, True, True, ["lu", ("row", h)], ["ps5"])
+        mm(T.ps6[:, 0:128], T.lp[0:25, :], r, True, True, ["lp", ("row", h)], ["ps6"])
+        if l:
+            es = T.es[:, h * 8:h * 8 + 8]
+            ttens(es, es, T.hd[:, h * 8:h * 8 + 8], A.add, [("es", h), ("hd", h)], [("es", h)])
+
+    def propose(t, l, h):
+        c = slice(h * 128, h * 128 + 128)
+        n = T.nm[:, (l + 1) * 256 + h * 128:(l + 1) * 256 + h * 128 + 128]
+        ttens(T.pt[:, c], T.ps5[:, 0:128], T.nc[:, c], A.mult, ["ps5", ("nc", h)], [("pt", h)])
+        yield
+        ttens(T.qt[:, c], T.ps6[:, 0:128], T.pt[:, c], A.add, ["ps6", ("pt", h)], [("qt", h)])
+        yield
+        tsc(n, T.qt[:, c], 6, A.arith_shift_right, [("qt", h)], [("nm", l + 1, h)], 4095, A.bitwise_and)
+        yield
+        tcopy(T.lst[:, lists(t, l + 1, h)], n, [("nm", l + 1, h)], [("L", t, l + 1, h)])
+        send(partner[t], T.clst[:, lists(t, l + 1, h)], T.lst[:, lists(t, l + 1, h)], "r%d_%d_%d" % (t, l + 1, h), [("L", t, l + 1, h)])
+        yield
+        if l < 3:
+            tsc(T.nc[:, c], n, -2048.0, A.add, [("nm", l + 1, h)], [("nc", h)])
+            yield
+
+    def copy_guesses():
+        for l in range(1, 4):
+            for h in range(2):
+                o = (l * 2 + h) * 24
+                i = T.tt[:, o + 8:o + 16]
+                d = T.h1[:, h * 32 + l:h * 32 + 32:4]
+                run("s", [("th", l, h)], [("h1x", l, h)], lambda e, i=i, d=d: e.activation(d, i, COPY))
+
+    def settle(t, part):
+        b = t * 80
+        HK = [("h1", 0)] + [("h1x", l, h) for l in range(1, 4) for h in range(2)]
+        DK = [("D", j, h) for j in range(4) for h in range(2)]
+        UK = [("U", j, h) for j in range(4) for h in range(2)]
+        e1 = ("e1", t)
+        m63 = slice(0, 63)
+        a = t * 64
+        if part == 0:
+            tsc(T.nh[:, :], T.h1[:, :], -1.0, A.mult, HK, ["nh"], 1.0, A.add)
+            tsc(T.lowa[:, :], T.uarr[:, :], 15, A.bitwise_and, UK + ["U"], ["lowa"])
+            ttens(T.he[:, :], T.h1[:, :], T.eqin[:, b:b + 64], A.mult, HK + [e1], ["he"])
+            tsc(T.low0[:, :], T.u0[:, :], 15, A.bitwise_and, [("u0", 0), ("u0", 1)], ["low0"])
+        elif part == 1:
+            scan(T.esq[:, :], T.nh[:, :], T.he[:, :], 0.0, A.mult, A.add, ["nh", "he"], ["esq"])
+            ttens(T.cod[:, :], T.lowa[:, :], T.c16[:, :], A.add, ["lowa", "c16"], ["cod"])
+            ttens(T.dq[:, m63], T.eqin[:, b + 1:b + 64], T.esq[:, m63], A.subtract, [e1, "esq"], ["dq"])
+            ttens(T.dtt[:, m63], T.dq[:, m63], T.darr[:, m63], A.add, ["dq", "D"] + DK, ["dtt"])
+            ttens(T.dd[:, m63], T.dtt[:, m63], T.a4[:, a:a + 63], A.is_le, ["dtt", "a4"], ["dd"])
+            ttens(T.ne[:, 1:64], T.dd[:, m63], T.h1[:, 1:64], A.not_equal, ["dd", "ne0"] + HK, ["ne"])
+            scan(T.wre[:, :], T.ne[:, 0:64], T.mk[:, :], 0.0, A.max, A.mult, ["ne", "ne0", "mk"], ["wre"])
+            ttens(T.go[:, m63], T.dd[:, m63], T.wre[:, m63], A.is_gt, ["dd", "wre"], ["go"])
+            tsc(T.nw[:, :], T.wre[:, 3::4], -1.0, A.mult, ["wre"], ["nw"], 1.0, A.add)
+            ttens(T.gco[:, m63], T.go[:, m63], T.cod[:, m63], A.mult, ["go", "cod"], ["gco"])
+            scan(T.sco[:, m63], T.mk[:, m63], T.gco[:, m63], 0.0, A.mult, A.max, ["mk", "gco"], ["sco"])
+            ttens(T.cp[:, :], T.sco[:, 2:63:4], T.low0[:, :], A.max, ["sco", "low0"], ["cp"])
+        else:
+            D3 = [("D", 3, 0), ("D", 3, 1)]
+            tsc(T.low4[:, :], T.uarr[:, 3::4], 15, A.bitwise_and, [("U", 3, 0), ("U", 3, 1)], ["low4"])
+            ttens(T.th0[:, :], T.a4[:, a + 3:a + 64:4], T.darr[:, 3::4], A.subtract, ["a4"] + D3, ["th0"])
+            tsc(T.cod4[:, :], T.low4[:, :], 64.0, A.add, ["low4"], ["cod4"])
+            ttens(T.thr[:, :], T.th0[:, :], T.esq[:, 3::4], A.add, ["th0", "esq"], ["thr"])
+            ttens(T.c4m[:, :], T.cod4[:, :], T.nw[:, :], A.mult, ["cod4", "nw"], ["c4m"])
+
+    def finish(t):
+        b = t * 80 + 64
+        last = t == RO - 1
+        ttens(T.d3[:, :], T.eqin[:, b:b + 16], T.thr[:, :], A.is_le, [("e2", t), "thr"], ["d3"])
+        ttens(T.gcx[:, :], T.d3[:, :], T.c4m[:, :], A.mult, ["d3", "c4m"], ["gcx"])
+        ttens(T.cd[:, :], T.gcx[:, :], T.cp[:, :], A.max, ["gcx", "cp"], ["cd"])
+        mm(T.ps4[0:16, 0:128], T.cd[:, :], T.idb[:, :], True, True, ["cd", "idb"], ["ps4"])
+        if not last:
+            ttens(T.ne3[:, :], T.d3[:, :], T.h3[:, :], A.not_equal, ["d3", ("h3", 0), ("h3", 1)], ["ne3"])
+        tcopy(T.rc[0:16, :], T.ps4[0:16, 0:128], ["ps4"], ["rc"])
+        for h in range(2):
+            mm(T.ps5[:, h * 128:h * 128 + 128], T.r8[0:16, h * 128:h * 128 + 128], T.rc[0:16, :], True, True, [("r8", h), "rc"], ["ps5"])
+        if not last:
+            ttens(T.wr[:, :], T.ne3[:, :], T.wre[:, 3::4], A.max, ["ne3", "wre"], ["wr"])
+            mm(T.ps7[:, 0:16], T.oneb[:, :], T.wr[:, :], True, True, ["oneb", "wr"], ["ps7"])
+        ttens(T.cm[:, :], T.ps5[:, 0:256], T.diag[:, :], A.mult, ["ps5", "diag"], ["cm"])
+        scan(T.lsc[:, :], T.mkx[:, 0:256], T.cm[:, :], 0.0, A.min, A.max, ["mkx", "cm"], ["lsc"])
+        tsc(T.ci[:, :], T.lsc[:, 15::16], 16.0, A.mult, ["lsc"], ["ci"])
+        tsc(T.ca[:, :], T.ci[:, :], 0x700, A.bitwise_and, ["ci"], ["ca"])
+        tsc(T.lo[:, :], T.ci[:, :], 4, A.arith_shift_right, ["ci"], ["lo"], 15, A.bitwise_and)
+        ttens(T.off[:, :], T.ca[:, :], T.ian[:, :], A.add, ["ca", "ian"], ["off"])
+        ttens(T.vi[:, :], T.lo[:, :], T.iav[:, :], A.add, ["lo", "iav"], ["vi"])
+        tsc(T.yl[:, :], T.off[:, :], 16.0, A.mult, ["off"], ["yl"], 15.0, A.add)
+        YK = [("y", l, h) for l in range(5) for h in range(2)]
+        run("s", YK + ["yl"], ["fy"], lambda e: e.activation(T.fy[:, :], T.ymax[:, :].indirect(T.yl[:, :]), COPY))
+        tcopy(T.nl[:, :], T.off[:, :], ["off"], ["nl"])
+        tcopy(T.vu[:, :], T.vi[:, :], ["vi"], ["vu"])
+        NK = [("nm", l, h) for l in range(5) for h in range(2)]
+        win = T.nm[:, :].indirect(T.nl[:, :])
+        if last:
+            tsc(T.vu[:, 8:16], T.vi[:, 8:16], -2048.0, A.add, ["vi", "vu"], ["vub"])
+            for h, q in ((0, "s"), (1, "y")):
+                c = slice(h * 128, h * 128 + 128)
+                half = T.tab[:, h * 2048:h * 2048 + 2048]
+                vl = half.indirect(T.vu[:, h * 8:h * 8 + 8])
+                ttens(T.sm[:, c], vl, T.fy[:, c], A.add, ["tab", "vu", "vub", "fy"], [("sm", h)])
+                tsc(T.sh[:, c], T.sm[:, c], 1, A.arith_shift_right, [("sm", h)], [("sh", h)])
+                V([("sh", h), "vu", "vub", "tab"], [("tabh", h)], lambda e, vl=vl, c=c: e.tensor_copy(vl, T.sh[:, c]))
+                run(q, [("tabh", h)], [], lambda e, h=h, half=half: e.dma_start(T.yx[:, h * 2048:h * 2048 + 2048], half), "stx%d" % h, 16)
+            tcopy(T.ycf[:, :], win, NK + ["nl"], ["ycf"])
+            run("y", ["ycf"], [], lambda e: e.dma_start(T.yc[:, :], T.ycf[:, :]), "stc", 16)
+        else:
+            tcopy(T.lst[:, lists(t + 1, 0)], win, NK + ["nl"], [("L", t + 1, 0, 0), ("L", t + 1, 0, 1)])
+            send_start(t + 1)
+            ttens(T.sm[:, :], T.tab[:, :].indirect(T.vu[:, :]), T.fy[:, :], A.add, ["tab", "vu", "fy"], [("sm", 0), ("sm", 1)])
+            tsc(T.sh[:, :], T.sm[:, :], 1, A.arith_shift_right, [("sm", 0)], [("sh", 0), ("sh", 1)])
+            V([("sh", 0), "vu"], ["tab"], lambda e: e.tensor_copy(T.tab[:, :].indirect(T.vu[:, :]), T.sh[:, :]))
+
+    def new_kappa():
+        V(["ps7"], ["ki0"], lambda e: e.tensor_reduce(T.kc[:, 1:2], T.ps7[:, 0:16], AxisListType.X, A.add))
+        tcopy(T.ki[:, 0:1], T.kc[:, 1:2], ["ki0"], ["ki1"])
+        tsc(T.ki[:, 1:2], T.ki[:, 0:1], 31, A.bitwise_and, ["ki1"], ["ki2"])
+        tcopy(T.kc[:, 0:1], T.ki[:, 1:2], ["ki2"], ["kc"])
+        kappa_rows()
+
+    for t in range(RO):
+        O = lambda l, h: ("o", t, l, h)
+        K = lambda l, h: ("c", t, l, h)
+        gather_own("s", t, 0, 0, 0)
+        gather_own("v", t, 0, 0, 1)
+        gather_own("s", t, 0, 1)
+        if t:
+            new_kappa()
+        start_names(t)
+        if t == 0:
+            constants_b()
+        for l in range(5):
+            if l:
+                gather_own("s", t, l, 0)
+                gather_client("s", t, l - 1, 1)
+            if 1 <= l <= 3:
+                gather_own("s", t, l, 1)
+            gather_client("s", t, l, 0)
+            if l == 4:
+                gather_client("s", t, 4, 1)
+                copy_guesses()
+                gather_own("s", t, 4, 1, 0)
+            scan_max(O(l, 0))
+            scan_min(O(l, 0))
+            if l:
+                scan_max(K(l - 1, 1))
+                scan_min(K(l - 1, 1))
+            weave(guess(t, l, 0), *([keep_spans(t, l - 1)] if l else []))
+            if l == 4:
+                return_spans(t, 0)
+                gather_own("v", t, 4, 1, 1)
+                for h in range(2):
+                    scan_max(K(4, h))
+                    scan_min(K(4, h))
+                settle(t, 0)
+                weave(keep_spans(t, 4))
+                return_spans(t, 1)
+                settle(t, 1)
+                scan_max(O(4, 1))
+                scan_min(O(4, 1))
+                weave(guess(t, 4, 1))
+                break
+            scan_max(O(l, 1))
+            rows(l, 0)
+            scan_min(O(l, 1))
+            weave(propose(t, l, 0), guess(t, l, 1))
+            if l == 0 and t == 0:
+                constants_c()
+            scan_max(K(l, 0))
+            rows(l, 1)
+            scan_min(K(l, 0))
+            weave(propose(t, l, 1))
+        settle(t, 2)
+        finish(t)
+    for s in sorted(total):
+        need("g", s, total[s])

@@ -3,13 +3,15 @@ from concourse.mybir import AluOpType, AxisListType, ActivationFunctionType
 RO = 3
 SEG = 2048
 NG = 6
+NP = 4
+N = SEG // NP
 
 SCRATCH = {}
 for _names, _d in (
-        ("tab:4096 gat:12288 ymax:20480 ymin:4096 cmax:4096 mkx:2048 mkn:2048 idb:128 oneb:128 rb1:16 rb2:16 rb3:16 r8:256 "
-         "diag:256 slb:256 per:96 cd:16 wr:16 rc:128 cm:256 lsc:256 fy:256", "bfloat16"),
+        ("tab:4096 gat:12288 ymax:20480 ymin:4096 cmax:4096 mkx:512 mkn:512 idb:128 oneb:128 rb1:16 rb2:16 rb3:16 r8:256 "
+         "diag:256 slb:256 per:96 cd:16 wr:16 rc:128 cm:256 mkl:256 fy:256", "bfloat16"),
         ("nm:1280 nc:256 qt:256 uarr:64 u0:16 um:16 ki:8 tmi:256 ian:16 iav:16 wti:1 wia:4 sli:256 lowa:64 low0:16 low4:16 "
-         "ci:16 ca:16 off:16 lo:16 vi:16 sm:256 sh:256", "int32"),
+         "lsc:256 ca:16 off:16 lo:16 vi:16 sm:256 sh:256", "int32"),
         ("lst:3840 clst:3840 nl:16 yl:16 vu:16", "uint16"),
         ("eret:240 eqin:240 pt:256 es:16 hd:16 darr:64 h1:64 h3:16 tt:240 row:256 lu:128 lp:128 sp:512 sx:256 k613:128 k77:8 "
          "kl:8 kc:4 one:128 idf:128 bo:8 mk:64 c16:64 wf:4 a4:192 nh:64 he:64 esq:64 dq:64 dtt:64 dd:64 ne:80 wre:64 go:64 "
@@ -158,6 +160,8 @@ def rank_program(g, core, T, topo):
     fill(T.uarr[:, :], 0, ["U"])
     fill(T.rb2[:, 0:8], 0.0, ["rb2"])
     fill(T.rb3[:, 8:16], 0.0, ["rb3b"])
+    fill(T.mkl[:, :], 1.0, ["mkl"])
+    fill(T.mkl[:, ::16], 0.0, ["mkl"])
     sel(T.bo[:, :], T.one[:, 0:8], [[-16, 8]], A.is_ge, 0.0, 0, 1, ["one"], ["bo"])
     sel(T.bo[:, :], T.bo[:, :], [[16, 8]], A.is_ge, 0.0, 15, -1, ["bo"], ["bo"])
     num(T.k77[:, 0:4], [[77, 4]], -77, 0, "k77")
@@ -213,7 +217,7 @@ def rank_program(g, core, T, topo):
         tcopy(T.idb[:, :], T.idf[:, :], ["idf"], ["idb"])
         tsc(T.tmi[:, :], T.tmi[:, :], 15, A.bitwise_and, ["tmi"], ["tmi"])
         tsc(T.ian[:, :], T.ian[:, :], 15, A.bitwise_and, ["ian"], ["ian"])
-        tsc(T.diag[:, :], T.tmi[:, :], 0.0, A.is_equal, ["tmi"], ["diag"])
+        tsc(T.diag[:, :], T.tmi[:, :], 0.0, A.is_equal, ["tmi"], ["diag"], 16.0, A.mult)
         ttens(T.ian[:, :], T.ian[:, :], T.iav[:, :], A.add, ["ian", "iav"], ["ian"])
         for h in range(2):
             tcopy(T.r8[0:16, h * 128:h * 128 + 128], T.sp[0:16, h * 128:h * 128 + 128], [("sp", h)], [("r8", h)])
@@ -228,59 +232,79 @@ def rank_program(g, core, T, topo):
 
     slot, mslot, where = [0], [0], {}
 
-    def gather(q, key, src, a, reads, part):
+    def gather(q, key, src, a, reads, p0, p1):
         if key not in where:
             slot[0] = (slot[0] + 1) % NG
             where[key] = slot[0]
         s = where[key]
-        p0, p1 = (0, 2) if part is None else (part, part + 1)
-        out = T.gat[:, s * SEG + p0 * SEG // 2:s * SEG + p1 * SEG // 2]
-        win = T.tab[:, :].indirect(src[:, a + p0 * 64:a + p1 * 64])
+        out = T.gat[:, s * SEG + p0 * N:s * SEG + p1 * N]
+        win = T.tab[:, :].indirect(src[:, a + p0 * 32:a + p1 * 32])
         keys = [("g", s, p) for p in range(p0, p1)]
         if q == "s":
             run("s", reads + ["tab"], keys, lambda e: e.activation(out, win, COPY))
         else:
             V(reads + ["tab"], keys, lambda e: e.tensor_copy(out, win))
 
-    def gather_own(q, t, l, h, part=None):
-        gather(q, ("o", t, l, h), T.lst, (t * 5 + l) * 256 + h * 128, [("L", t, l, h)], part)
+    def gather_own(q, t, l, h, p0=0, p1=4):
+        gather(q, ("o", t, l, h), T.lst, (t * 5 + l) * 256 + h * 128, [("L", t, l, h)], p0, p1)
 
-    def gather_client(q, t, l, h, part=None):
-        gather(q, ("c", t, l, h), T.clst, (t * 5 + l) * 256 + h * 128, [("cl", t, 0) if l == 0 else ("cl", t, l, h)], part)
+    def shared(l, h):
+        return h == 1 and l < 4
 
-    def scan_max(key):
-        s = where[key]
-        kind, t, l, h = key
-        out, kk = (T.ymax[:, l * 4096 + h * SEG:l * 4096 + (h + 1) * SEG], ("y", l, h)) if kind == "o" else \
-            (T.cmax[:, h * SEG:(h + 1) * SEG], ("cy", h))
-        scan(out, T.mkx[:, :], T.gat[:, s * SEG:(s + 1) * SEG], 0.0, A.min, A.max, ["mkx", ("g", s, 0), ("g", s, 1)], [kk])
+    def gather_client(q, t, l, h, p0=0, p1=4):
+        if q == "s" and shared(l, h):
+            p1 = 3
+        gather(q, ("c", t, l, h), T.clst, (t * 5 + l) * 256 + h * 128, [("cl", t, 0) if l == 0 else ("cl", t, l, h)], p0, p1)
 
-    def scan_min(key):
+    def scans(key):
         s = where[key]
         kind, t, l, h = key
         m = mslot[0] = mslot[0] ^ 1
-        scan(T.ymin[:, m * SEG:(m + 1) * SEG], T.mkn[:, :], T.gat[:, s * SEG:(s + 1) * SEG], 255.0, A.max, A.min,
-             ["mkn", ("g", s, 0), ("g", s, 1)], [("m", m)])
-        mn = T.ymin[:, m * SEG + 15:(m + 1) * SEG:16]
+        buf, y0, yk = (T.ymax, l * 4096 + h * SEG, ("y", l, h)) if kind == "o" else (T.cmax, h * SEG, ("cy", h))
+        if kind == "c" and shared(l, h):
+            gather_client("v", t, l, h, 3, 4)
+            yield
+        for p in range(NP):
+            x = T.gat[:, s * SEG + p * N:s * SEG + p * N + N]
+            scan(buf[:, y0 + p * N:y0 + p * N + N], T.mkx[:, :], x, 0.0, A.min, A.max, ["mkx", ("g", s, p)], [yk + (p,)])
+            yield
+        for p in range(NP):
+            x = T.gat[:, s * SEG + p * N:s * SEG + p * N + N]
+            scan(T.ymin[:, m * SEG + p * N:m * SEG + p * N + N], T.mkn[:, :], x, 255.0, A.max, A.min, ["mkn", ("g", s, p)], [("m", m, p)])
+            if p < NP - 1:
+                yield
+        y, mn = buf[:, y0 + 15:y0 + SEG:16], T.ymin[:, m * SEG + 15:(m + 1) * SEG:16]
+        YP, MP = [yk + (p,) for p in range(NP)], [("m", m, p) for p in range(NP)]
         if kind == "o":
             b = "ps%d" % h
-            y0 = l * 4096 + h * SEG
-            y = T.ymax[:, y0 + 15:y0 + SEG:16]
             out = T[b][:, 0:16]
-            mm(out, y, T.rb1[:, :], True, False, ["rb1", "rb1b", ("y", l, h)], [b])
-            mm(out, y, T.rb2[:, :], False, False, ["rb2", "rb2b", ("y", l, h)], [b])
-            mm(out, mn, T.rb3[:, :], False, True, ["rb3", "rb3b", ("m", m)], [b])
+            mm(out, y, T.rb1[:, :], True, False, ["rb1", "rb1b"] + YP, [b])
+            mm(out, y, T.rb2[:, :], False, False, ["rb2", "rb2b"] + YP, [b])
+            mm(out, mn, T.rb3[:, :], False, True, ["rb3", "rb3b"] + MP, [b])
         else:
-            y = T.cmax[:, h * SEG + 15:(h + 1) * SEG:16]
             out = T.ps2[:, h * 8:h * 8 + 8]
-            mm(out, y, T.rb1[:, 0:8], True, False, ["rb1", ("cy", h)], ["ps2"])
-            mm(out, mn, T.rb3[:, 0:8], False, True, ["rb3", ("m", m)], ["ps2"])
+            mm(out, y, T.rb1[:, 0:8], True, False, ["rb1"] + YP, ["ps2"])
+            mm(out, mn, T.rb3[:, 0:8], False, True, ["rb3"] + MP, ["ps2"])
+        yield
+
+    def stream(*keys):
+        for key in keys:
+            for _ in scans(key):
+                yield
+
+    def drive(chain, filler):
+        for k in chain:
+            for _ in range(k):
+                next(filler, None)
+
+    def drain(filler):
+        for _ in filler:
+            pass
 
     def keep_spans(t, l):
         a = t * 80
         o = T.eret[:, a + l:a + 64:4] if l < 4 else T.eret[:, a + 64:a + 80]
         tcopy(o, T.ps2[:, 0:16], ["ps2"], [("er", t, l)])
-        yield
 
     def return_spans(t, part):
         a = t * 80 + (64 if part else 0)
@@ -288,83 +312,66 @@ def rank_program(g, core, T, topo):
         ls = [4] if part else range(4)
         send(client[t], T.eqin[:, a:a + n], T.eret[:, a:a + n], "e%d_%d" % (part + 1, t), [("er", t, l) for l in ls])
 
-    def weave(*parts):
-        live = list(parts)
-        while live:
-            for x in list(live):
-                if next(x, "end") == "end":
-                    live.remove(x)
-
-    def guess(t, l, h):
+    def step(t, l, h, keep):
+        c = slice(h * 128, h * 128 + 128)
         b = "ps%d" % h
         E, U = T[b][:, 0:8], T[b][:, 8:16]
-        es = T.es[:, h * 8:h * 8 + 8]
+        es, hd = T.es[:, h * 8:h * 8 + 8], T.hd[:, h * 8:h * 8 + 8]
         um = T.um[:, h * 8:h * 8 + 8]
         o = (l * 2 + h) * 24
         H = T.tt[:, o + 8:o + 16]
         j = l - 1
-        if l == 0:
-            u0 = T.u0[:, h * 8:h * 8 + 8]
-            tcopy(u0, U, [b], [("u0", h)])
-            yield
-            fill(H, 1.0, [("th", 0, h)])
-            yield
-            tsc(um, u0, 4095, A.bitwise_and, [("u0", h)], [("um", h)])
-            yield
-            tcopy(es, E, [b], [("es", h)])
-            yield
-            tcopy(T.tt[:, o:o + 8], um, [("um", h)], [("tu", 0, h)])
-            yield
-        else:
+        yield 2
+        if l:
             D = T.darr[:, h * 32 + j:h * 32 + 32:4]
             Ua = T.uarr[:, h * 32 + j:h * 32 + 32:4]
             a = T.a4[:, t * 64 + h * 32 + j:t * 64 + h * 32 + 32:4]
             ttens(D, E, es, A.subtract, [b, ("es", h), "D"], [("D", j, h)])
-            yield
             tcopy(Ua, U, [b, "U"], [("U", j, h)])
-            yield
+            yield 1
             if l == 4:
                 ttens(T.h3[:, h * 8:h * 8 + 8], D, a, A.is_le, [("D", j, h), "a4"], [("h3", h)])
                 return
             ttens(H, D, a, A.is_le, [("D", j, h), "a4"], [("th", l, h)])
-            yield
             tsc(um, Ua, 4095, A.bitwise_and, [("U", j, h)], [("um", h)])
-            yield
-        tsc(T.tt[:, o + 16:o + 24], H, T.kl[:, l:l + 1], A.mult, [("th", l, h), "kl"], [("tk", l, h)])
-        yield
-        if l:
+            yield 1
+            tsc(T.tt[:, o + 16:o + 24], H, T.kl[:, l:l + 1], A.mult, [("th", l, h), "kl"], [("tk", l, h)])
             ttens(T.tt[:, o:o + 8], um, H, A.mult, [("um", h), ("th", l, h)], [("tu", l, h)])
-        mm(T.ps4[0:24, h * 128:h * 128 + 128], T.tt[:, o:o + 24], T.idf[:, :], True, True,
-           [("tu", l, h), ("th", l, h), ("tk", l, h), "idf"], ["ps4"])
-        yield
+        else:
+            u0 = T.u0[:, h * 8:h * 8 + 8]
+            tcopy(u0, U, [b], [("u0", h)])
+            fill(H, 1.0, [("th", 0, h)])
+            tcopy(es, E, [b], [("es", h)])
+            yield 1
+            tsc(um, u0, 4095, A.bitwise_and, [("u0", h)], [("um", h)])
+            tsc(T.tt[:, o + 16:o + 24], H, T.kl[:, 0:1], A.mult, [("th", l, h), "kl"], [("tk", l, h)])
+            yield 1
+            tcopy(T.tt[:, o:o + 8], um, [("um", h)], [("tu", 0, h)])
+        mm(T.ps4[0:24, c], T.tt[:, o:o + 24], T.idf[:, :], True, True, [("tu", l, h), ("th", l, h), ("tk", l, h), "idf"], ["ps4"])
         if l:
-            ttens(T.hd[:, h * 8:h * 8 + 8], H, D, A.mult, [("th", l, h), ("D", j, h)], [("hd", h)])
-            yield
-
-    def rows(l, h):
-        r = T.row[0:25, h * 128:h * 128 + 128]
-        tcopy(T.row[0:24, h * 128:h * 128 + 128], T.ps4[0:24, h * 128:h * 128 + 128], ["ps4"], [("row", h)])
+            ttens(hd, H, D, A.mult, [("th", l, h), ("D", j, h)], [("hd", h)])
+        yield 3
+        r = T.row[0:25, c]
+        tcopy(T.row[0:24, c], T.ps4[0:24, c], ["ps4"], [("row", h)])
         mm(T.ps5[:, 0:128], T.lu[0:25, :], r, True, True, ["lu", ("row", h)], ["ps5"])
         mm(T.ps6[:, 0:128], T.lp[0:25, :], r, True, True, ["lp", ("row", h)], ["ps6"])
         if l:
-            es = T.es[:, h * 8:h * 8 + 8]
-            ttens(es, es, T.hd[:, h * 8:h * 8 + 8], A.add, [("es", h), ("hd", h)], [("es", h)])
-
-    def propose(t, l, h):
-        c = slice(h * 128, h * 128 + 128)
+            ttens(es, es, hd, A.add, [("es", h), ("hd", h)], [("es", h)])
+        yield 3
         n = T.nm[:, (l + 1) * 256 + h * 128:(l + 1) * 256 + h * 128 + 128]
+        L = T.lst[:, lists(t, l + 1, h)]
         ttens(T.pt[:, c], T.ps5[:, 0:128], T.nc[:, c], A.mult, ["ps5", ("nc", h)], [("pt", h)])
-        yield
+        yield 1
         ttens(T.qt[:, c], T.ps6[:, 0:128], T.pt[:, c], A.add, ["ps6", ("pt", h)], [("qt", h)])
-        yield
+        if keep:
+            keep_spans(t, l - 1)
+        yield 1
         tsc(n, T.qt[:, c], 6, A.arith_shift_right, [("qt", h)], [("nm", l + 1, h)], 4095, A.bitwise_and)
-        yield
-        tcopy(T.lst[:, lists(t, l + 1, h)], n, [("nm", l + 1, h)], [("L", t, l + 1, h)])
-        send(partner[t], T.clst[:, lists(t, l + 1, h)], T.lst[:, lists(t, l + 1, h)], "r%d_%d_%d" % (t, l + 1, h), [("L", t, l + 1, h)])
-        yield
+        yield 1
+        tcopy(L, n, [("nm", l + 1, h)], [("L", t, l + 1, h)])
+        send(partner[t], T.clst[:, lists(t, l + 1, h)], L, "r%d_%d_%d" % (t, l + 1, h), [("L", t, l + 1, h)])
         if l < 3:
             tsc(T.nc[:, c], n, -2048.0, A.add, [("nm", l + 1, h)], [("nc", h)])
-            yield
 
     def copy_guesses():
         for l in range(1, 4):
@@ -374,7 +381,7 @@ def rank_program(g, core, T, topo):
                 d = T.h1[:, h * 32 + l:h * 32 + 32:4]
                 run("s", [("th", l, h)], [("h1x", l, h)], lambda e, i=i, d=d: e.activation(d, i, COPY))
 
-    def settle(t, part):
+    def settle(t):
         b = t * 80
         HK = [("h1", 0)] + [("h1x", l, h) for l in range(1, 4) for h in range(2)]
         DK = [("D", j, h) for j in range(4) for h in range(2)]
@@ -382,31 +389,39 @@ def rank_program(g, core, T, topo):
         e1 = ("e1", t)
         m63 = slice(0, 63)
         a = t * 64
-        if part == 0:
-            tsc(T.nh[:, :], T.h1[:, :], -1.0, A.mult, HK, ["nh"], 1.0, A.add)
-            tsc(T.lowa[:, :], T.uarr[:, :], 15, A.bitwise_and, UK + ["U"], ["lowa"])
-            ttens(T.he[:, :], T.h1[:, :], T.eqin[:, b:b + 64], A.mult, HK + [e1], ["he"])
-            tsc(T.low0[:, :], T.u0[:, :], 15, A.bitwise_and, [("u0", 0), ("u0", 1)], ["low0"])
-        elif part == 1:
-            scan(T.esq[:, :], T.nh[:, :], T.he[:, :], 0.0, A.mult, A.add, ["nh", "he"], ["esq"])
-            ttens(T.cod[:, :], T.lowa[:, :], T.c16[:, :], A.add, ["lowa", "c16"], ["cod"])
-            ttens(T.dq[:, m63], T.eqin[:, b + 1:b + 64], T.esq[:, m63], A.subtract, [e1, "esq"], ["dq"])
-            ttens(T.dtt[:, m63], T.dq[:, m63], T.darr[:, m63], A.add, ["dq", "D"] + DK, ["dtt"])
-            ttens(T.dd[:, m63], T.dtt[:, m63], T.a4[:, a:a + 63], A.is_le, ["dtt", "a4"], ["dd"])
-            ttens(T.ne[:, 1:64], T.dd[:, m63], T.h1[:, 1:64], A.not_equal, ["dd", "ne0"] + HK, ["ne"])
-            scan(T.wre[:, :], T.ne[:, 0:64], T.mk[:, :], 0.0, A.max, A.mult, ["ne", "ne0", "mk"], ["wre"])
-            ttens(T.go[:, m63], T.dd[:, m63], T.wre[:, m63], A.is_gt, ["dd", "wre"], ["go"])
-            tsc(T.nw[:, :], T.wre[:, 3::4], -1.0, A.mult, ["wre"], ["nw"], 1.0, A.add)
-            ttens(T.gco[:, m63], T.go[:, m63], T.cod[:, m63], A.mult, ["go", "cod"], ["gco"])
-            scan(T.sco[:, m63], T.mk[:, m63], T.gco[:, m63], 0.0, A.mult, A.max, ["mk", "gco"], ["sco"])
-            ttens(T.cp[:, :], T.sco[:, 2:63:4], T.low0[:, :], A.max, ["sco", "low0"], ["cp"])
-        else:
-            D3 = [("D", 3, 0), ("D", 3, 1)]
-            tsc(T.low4[:, :], T.uarr[:, 3::4], 15, A.bitwise_and, [("U", 3, 0), ("U", 3, 1)], ["low4"])
-            ttens(T.th0[:, :], T.a4[:, a + 3:a + 64:4], T.darr[:, 3::4], A.subtract, ["a4"] + D3, ["th0"])
-            tsc(T.cod4[:, :], T.low4[:, :], 64.0, A.add, ["low4"], ["cod4"])
-            ttens(T.thr[:, :], T.th0[:, :], T.esq[:, 3::4], A.add, ["th0", "esq"], ["thr"])
-            ttens(T.c4m[:, :], T.cod4[:, :], T.nw[:, :], A.mult, ["cod4", "nw"], ["c4m"])
+        tsc(T.nh[:, :], T.h1[:, :], -1.0, A.mult, HK, ["nh"], 1.0, A.add)
+        tsc(T.lowa[:, :], T.uarr[:, :], 15, A.bitwise_and, UK + ["U"], ["lowa"])
+        tsc(T.low0[:, :], T.u0[:, :], 15, A.bitwise_and, [("u0", 0), ("u0", 1)], ["low0"])
+        yield 1
+        ttens(T.cod[:, :], T.lowa[:, :], T.c16[:, :], A.add, ["lowa", "c16"], ["cod"])
+        yield 1
+        ttens(T.he[:, :], T.h1[:, :], T.eqin[:, b:b + 64], A.mult, HK + [e1], ["he"])
+        yield 1
+        keep_spans(t, 4)
+        return_spans(t, 1)
+        scan(T.esq[:, :], T.nh[:, :], T.he[:, :], 0.0, A.mult, A.add, ["nh", "he"], ["esq"])
+        yield 1
+        ttens(T.dq[:, m63], T.eqin[:, b + 1:b + 64], T.esq[:, m63], A.subtract, [e1, "esq"], ["dq"])
+        yield 1
+        ttens(T.dtt[:, m63], T.dq[:, m63], T.darr[:, m63], A.add, ["dq", "D"] + DK, ["dtt"])
+        yield 1
+        ttens(T.dd[:, m63], T.dtt[:, m63], T.a4[:, a:a + 63], A.is_le, ["dtt", "a4"], ["dd"])
+        yield 1
+        ttens(T.ne[:, 1:64], T.dd[:, m63], T.h1[:, 1:64], A.not_equal, ["dd", "ne0"] + HK, ["ne"])
+        yield 2
+        scan(T.wre[:, :], T.ne[:, 0:64], T.mk[:, :], 0.0, A.max, A.mult, ["ne", "ne0", "mk"], ["wre"])
+        for _ in step(t, 4, 1, False):
+            pass
+        ttens(T.go[:, m63], T.dd[:, m63], T.wre[:, m63], A.is_gt, ["dd", "wre"], ["go"])
+        tsc(T.nw[:, :], T.wre[:, 3::4], -1.0, A.mult, ["wre"], ["nw"], 1.0, A.add)
+        tsc(T.low4[:, :], T.uarr[:, 3::4], 15, A.bitwise_and, [("U", 3, 0), ("U", 3, 1)], ["low4"])
+        ttens(T.gco[:, m63], T.go[:, m63], T.cod[:, m63], A.mult, ["go", "cod"], ["gco"])
+        ttens(T.th0[:, :], T.a4[:, a + 3:a + 64:4], T.darr[:, 3::4], A.subtract, ["a4", ("D", 3, 0), ("D", 3, 1)], ["th0"])
+        tsc(T.cod4[:, :], T.low4[:, :], 64.0, A.add, ["low4"], ["cod4"])
+        scan(T.sco[:, m63], T.mk[:, m63], T.gco[:, m63], 0.0, A.mult, A.max, ["mk", "gco"], ["sco"])
+        ttens(T.thr[:, :], T.th0[:, :], T.esq[:, 3::4], A.add, ["th0", "esq"], ["thr"])
+        ttens(T.c4m[:, :], T.cod4[:, :], T.nw[:, :], A.mult, ["cod4", "nw"], ["c4m"])
+        ttens(T.cp[:, :], T.sco[:, 2:63:4], T.low0[:, :], A.max, ["sco", "low0"], ["cp"])
 
     def finish(t):
         b = t * 80 + 64
@@ -424,14 +439,14 @@ def rank_program(g, core, T, topo):
             ttens(T.wr[:, :], T.ne3[:, :], T.wre[:, 3::4], A.max, ["ne3", "wre"], ["wr"])
             mm(T.ps7[:, 0:16], T.oneb[:, :], T.wr[:, :], True, True, ["oneb", "wr"], ["ps7"])
         ttens(T.cm[:, :], T.ps5[:, 0:256], T.diag[:, :], A.mult, ["ps5", "diag"], ["cm"])
-        scan(T.lsc[:, :], T.mkx[:, 0:256], T.cm[:, :], 0.0, A.min, A.max, ["mkx", "cm"], ["lsc"])
-        tsc(T.ci[:, :], T.lsc[:, 15::16], 16.0, A.mult, ["lsc"], ["ci"])
-        tsc(T.ca[:, :], T.ci[:, :], 0x700, A.bitwise_and, ["ci"], ["ca"])
-        tsc(T.lo[:, :], T.ci[:, :], 4, A.arith_shift_right, ["ci"], ["lo"], 15, A.bitwise_and)
+        scan(T.lsc[:, :], T.mkl[:, :], T.cm[:, :], 0.0, A.mult, A.max, ["mkl", "cm"], ["lsc"])
+        ci = T.lsc[:, 15::16]
+        tsc(T.ca[:, :], ci, 0x700, A.bitwise_and, ["lsc"], ["ca"])
+        tsc(T.lo[:, :], ci, 4, A.arith_shift_right, ["lsc"], ["lo"], 15, A.bitwise_and)
         ttens(T.off[:, :], T.ca[:, :], T.ian[:, :], A.add, ["ca", "ian"], ["off"])
         ttens(T.vi[:, :], T.lo[:, :], T.iav[:, :], A.add, ["lo", "iav"], ["vi"])
         tsc(T.yl[:, :], T.off[:, :], 16.0, A.mult, ["off"], ["yl"], 15.0, A.add)
-        YK = [("y", l, h) for l in range(5) for h in range(2)]
+        YK = [("y", l, h, p) for l in range(5) for h in range(2) for p in range(NP)]
         run("s", YK + ["yl"], ["fy"], lambda e: e.activation(T.fy[:, :], T.ymax[:, :].indirect(T.yl[:, :]), COPY))
         tcopy(T.nl[:, :], T.off[:, :], ["off"], ["nl"])
         tcopy(T.vu[:, :], T.vi[:, :], ["vi"], ["vu"])
@@ -458,64 +473,58 @@ def rank_program(g, core, T, topo):
 
     def new_kappa():
         V(["ps7"], ["ki0"], lambda e: e.tensor_reduce(T.kc[:, 1:2], T.ps7[:, 0:16], AxisListType.X, A.add))
+        yield 1
         tcopy(T.ki[:, 0:1], T.kc[:, 1:2], ["ki0"], ["ki1"])
+        yield 1
         tsc(T.ki[:, 1:2], T.ki[:, 0:1], 31, A.bitwise_and, ["ki1"], ["ki2"])
+        yield 1
         tcopy(T.kc[:, 0:1], T.ki[:, 1:2], ["ki2"], ["kc"])
+        yield 1
         kappa_rows()
 
     for t in range(RO):
         O = lambda l, h: ("o", t, l, h)
         K = lambda l, h: ("c", t, l, h)
-        gather_own("s", t, 0, 0, 0)
-        gather_own("v", t, 0, 0, 1)
+        gather_own("s", t, 0, 0, 0, 2)
+        gather_own("v", t, 0, 0, 2, 4)
         gather_own("s", t, 0, 1)
+        gather_client("s", t, 0, 0)
+        first = stream(O(0, 0))
         if t:
-            new_kappa()
+            drive(new_kappa(), first)
         start_names(t)
         if t == 0:
             constants_b()
-        for l in range(5):
-            if l:
-                gather_own("s", t, l, 0)
-                gather_client("s", t, l - 1, 1)
-            if 1 <= l <= 3:
-                gather_own("s", t, l, 1)
-            gather_client("s", t, l, 0)
-            if l == 4:
-                gather_client("s", t, 4, 1)
-                copy_guesses()
-                gather_own("s", t, 4, 1, 0)
-            scan_max(O(l, 0))
-            scan_min(O(l, 0))
-            if l:
-                scan_max(K(l - 1, 1))
-                scan_min(K(l - 1, 1))
-            weave(guess(t, l, 0), *([keep_spans(t, l - 1)] if l else []))
-            if l == 4:
-                return_spans(t, 0)
-                gather_own("v", t, 4, 1, 1)
-                for h in range(2):
-                    scan_max(K(4, h))
-                    scan_min(K(4, h))
-                settle(t, 0)
-                weave(keep_spans(t, 4))
-                return_spans(t, 1)
-                settle(t, 1)
-                scan_max(O(4, 1))
-                scan_min(O(4, 1))
-                weave(guess(t, 4, 1))
-                break
-            scan_max(O(l, 1))
-            rows(l, 0)
-            scan_min(O(l, 1))
-            weave(propose(t, l, 0), guess(t, l, 1))
+        drain(first)
+        for l in range(4):
+            f = stream(*([K(l - 1, 1)] if l else []), O(l, 1))
+            drive(step(t, l, 0, l > 0), f)
+            gather_own("s", t, l + 1, 0)
+            gather_client("s", t, l, 1)
+            drain(f)
             if l == 0 and t == 0:
                 constants_c()
-            scan_max(K(l, 0))
-            rows(l, 1)
-            scan_min(K(l, 0))
-            weave(propose(t, l, 1))
-        settle(t, 2)
+            f = stream(K(l, 0), O(l + 1, 0))
+            drive(step(t, l, 1, False), f)
+            if l < 3:
+                gather_own("s", t, l + 1, 1)
+            gather_client("s", t, l + 1, 0)
+            drain(f)
+        gather_client("s", t, 4, 1)
+        copy_guesses()
+        gather_own("s", t, 4, 1, 0, 2)
+        f = stream(K(3, 1), K(4, 0))
+        drive(step(t, 4, 0, False), f)
+        for _ in range(2 * NP):
+            next(f)
+        keep_spans(t, 3)
+        return_spans(t, 0)
+        gather_own("v", t, 4, 1, 2, 4)
+        drain(f)
+        drain(stream(K(4, 1)))
+        f = stream(O(4, 1))
+        drive(settle(t), f)
+        drain(f)
         finish(t)
     for s in sorted(total):
         need("g", s, total[s])

from concourse.mybir import AluOpType, AxisListType, ActivationFunctionType

RO = 3
SEG = 2048
NG = 6
NP = 4
N = SEG // NP

SCRATCH = {}
for _names, _d in (
        ("tab:4096 gat:12288 ymax:20480 ymin:4096 cmax:4096 mkx:512 mkn:512 idb:128 oneb:128 rb1:16 rb2:16 rb3:16 r8:256 "
         "diag:256 slb:256 per:96 cd:16 wr:16 rc:128 cm:256 mkl:256 fy:256", "bfloat16"),
        ("nm:1280 nc:256 qt:256 uarr:64 u0:16 um:16 ki:8 tmi:256 ian:16 iav:16 wti:1 wia:4 sli:256 lowa:64 low0:16 low4:16 "
         "lsc:256 ca:16 off:16 lo:16 vi:16 sm:256 sh:256", "int32"),
        ("lst:3840 clst:3840 nl:16 yl:16 vu:16", "uint16"),
        ("eret:240 eqin:240 pt:256 es:16 hd:16 darr:64 h1:64 h3:16 tt:240 row:256 lu:128 lp:128 sp:512 sx:256 k613:128 k77:8 "
         "kl:8 kc:4 one:128 idf:128 bo:8 mk:64 c16:64 wf:4 a4:192 nh:64 he:64 esq:64 dq:64 dtt:64 dd:64 ne:80 wre:64 go:64 "
         "cod:64 cod4:16 gco:64 sco:64 cp:16 th0:16 thr:16 nw:16 c4m:16 d3:16 gcx:16 ne3:16 ycf:256", "float32")):
    for _n in _names.split():
        SCRATCH[_n.split(":")[0]] = ("sbuf", [128, int(_n.split(":")[1])], _d)
for _b in range(8):
    SCRATCH["ps%d" % _b] = ("psum", [128, 512], "float32")

SEMAPHORES = ["v_q", "s_q", "p_q", "g_q", "snt", "ldc", "ldx", "ldw", "ldl", "stc", "stx0", "stx1"]
for _t in range(RO):
    SEMAPHORES += ["r%d_0" % _t, "e1_%d" % _t, "e2_%d" % _t]
    for _l in range(1, 5):
        SEMAPHORES += ["r%d_%d_%d" % (_t, _l, _h) for _h in range(2)]


def rank_program(g, core, T, topo):
    rank = T.rank_of(core)
    if rank is None:
        return
    n_ranks = len(T.cores)
    A, COPY = AluOpType, ActivationFunctionType.Copy
    eng = {"v": g.vector, "s": g.scalar, "p": g.tensor, "g": g, "y": g.sync}
    know = {q: {} for q in eng}
    snap = {}
    total = {}
    wrote, red = {}, {}

    def need(q, s, c):
        if know[q].get(s, 0) >= c:
            return
        eng[q].wait_ge(T.sem[s], c)
        know[q][s] = c
        for s2, c2 in snap.get((s, c), {}).items():
            know[q][s2] = max(know[q].get(s2, 0), c2)

    def pre(q, reads, writes):
        want = {}
        for k in list(reads) + list(writes):
            if k in wrote and not (q == "p" and wrote[k][0] == "p_q"):
                s, c = wrote[k]
                want[s] = max(want.get(s, 0), c)
        for k in writes:
            for s, c in red.get(k, {}).items():
                want[s] = max(want.get(s, 0), c)
        order = sorted(want, key=lambda s: (s == q + "_q", s))
        full = {s: snap.get((s, want[s]), {}) for s in order}
        for s in order:
            if not any(full[o].get(s, 0) >= want[s] and full[s].get(o, 0) < want[o] for o in order if o != s):
                need(q, s, want[s])
        for s in order:
            need(q, s, want[s])

    def run(q, reads, writes, fn, sem=None, inc=1):
        pre(q, reads, writes)
        s = sem or q + "_q"
        c = total[s] = total.get(s, 0) + inc
        fn(eng[q]).then_inc(T.sem[s], inc)
        snap[(s, c)] = dict(know[q])
        snap[(s, c)][s] = c
        for k in reads:
            red.setdefault(k, {})[s] = c
        for k in writes:
            wrote[k] = (s, c)
            red[k] = {}

    def V(reads, writes, fn):
        run("v", reads, writes, fn)

    def tcopy(out, in_, reads, writes):
        V(reads, writes, lambda e: e.tensor_copy(out, in_))

    def ttens(out, a, b, op, reads, writes):
        V(reads, writes, lambda e: e.tensor_tensor(out, a, b, op))

    def tsc(out, a, s1, op0, reads, writes, s2=None, op1=None):
        if op1 is None:
            V(reads, writes, lambda e: e.tensor_scalar(out, a, s1, None, op0))
        else:
            V(reads, writes, lambda e: e.tensor_scalar(out, a, s1, s2, op0, op1))

    def scan(out, d0, d1, init, o0, o1, reads, writes):
        V(reads, writes, lambda e: e.tensor_tensor_scan(out, d0, d1, init, o0, o1))

    def fill(ap, x, writes):
        V([], writes, lambda e: e.memset(ap, x))

    def mm(out, lhsT, rhs, start, stop, reads, writes):
        run("p", reads, writes, lambda e: e.matmul(out, lhsT, rhs, start, stop))

    def sel(out, in_, pattern, op, fillv, base, cm, reads, writes):
        run("g", reads, writes, lambda e: e.affine_select(out, in_, pattern, op, fillv, base, cm))

    def num(ap, pattern, base, cm, key):
        run("g", [], [key], lambda e: e.iota(ap, pattern, base, cm, allow_small_or_imprecise_dtypes=True))

    def send(dst, out, in_, rsem, reads):
        pre("g", reads, [])
        rid, pid, _ = topo.addr(dst)
        g.remote_dma(out, in_, T.sem[rsem], T.sem["snt"], pid, rid, topo.mask(core, dst))
        total["snt"] = total.get("snt", 0) + len(topo.engines(core, dst))

    def arrives(key, s, src):
        c = total[s] = len(topo.engines(src, core))
        wrote[key] = (s, c)

    run("y", [], [("nm", 0, 0), ("nm", 0, 1)], lambda e: e.dma_start(T.nm[:, 0:256], T.ch[:, :]), "ldc", 16)
    run("s", [], ["tab"], lambda e: e.dma_start(T.tab[:, :], T.xt[:, :]), "ldx", 16)
    run("y", [], ["wti"], lambda e: e.dma_start(T.wti[:, :], T.wt[:, :]), "ldw", 16)
    for i in range(2):
        g.sync.dma_start(T.sli[0:96, i * 128:(i + 1) * 128], T.sl[4 * i:4 * i + 4, :]).then_inc(T.sem["ldl"], 16)
    total["ldl"] = 32
    wrote["sli"] = ("ldl", 32)

    def lists(t, l, h=None):
        a = (t * 5 + l) * 256
        return slice(a, a + 256) if h is None else slice(a + h * 128, a + h * 128 + 128)

    partner = [T.cores[(rank + 1 + t % (n_ranks - 1)) % n_ranks] for t in range(RO)]
    client = [T.cores[(rank - 1 - t % (n_ranks - 1)) % n_ranks] for t in range(RO)]
    for t in range(RO):
        arrives(("cl", t, 0), "r%d_0" % t, client[t])
        for l in range(1, 5):
            for h in range(2):
                arrives(("cl", t, l, h), "r%d_%d_%d" % (t, l, h), client[t])
        arrives(("e1", t), "e1_%d" % t, partner[t])
        arrives(("e2", t), "e2_%d" % t, partner[t])

    def send_start(t):
        send(partner[t], T.clst[:, lists(t, 0)], T.lst[:, lists(t, 0)], "r%d_0" % t, [("L", t, 0, 0), ("L", t, 0, 1)])

    fill(T.one[:, :], 1.0, ["one"])
    tcopy(T.lst[:, lists(0, 0)], T.nm[:, 0:256], [("nm", 0, 0), ("nm", 0, 1)], [("L", 0, 0, 0), ("L", 0, 0, 1)])
    fill(T.mkx[:, :], 255.0, ["mkx"])
    fill(T.mkx[:, ::16], 0.0, ["mkx"])
    fill(T.mkn[:, :], 0.0, ["mkn"])
    fill(T.mkn[:, ::16], 255.0, ["mkn"])
    fill(T.oneb[:, :], 1.0, ["oneb"])
    fill(T.row[:, :], 1.0, [("row", 0), ("row", 1)])
    fill(T.kc[:, :], 0.0, ["kc"])
    fill(T.mk[:, :], 1.0, ["mk"])
    fill(T.mk[:, ::4], 0.0, ["mk"])
    fill(T.h1[:, ::4], 1.0, [("h1", 0)])
    fill(T.ne[:, 0:16], 0.0, ["ne0"])
    fill(T.darr[:, :], 0.0, ["D"])
    fill(T.uarr[:, :], 0, ["U"])
    fill(T.rb2[:, 0:8], 0.0, ["rb2"])
    fill(T.rb3[:, 8:16], 0.0, ["rb3b"])
    fill(T.mkl[:, :], 1.0, ["mkl"])
    fill(T.mkl[:, ::16], 0.0, ["mkl"])
    sel(T.bo[:, :], T.one[:, 0:8], [[-16, 8]], A.is_ge, 0.0, 0, 1, ["one"], ["bo"])
    sel(T.bo[:, :], T.bo[:, :], [[16, 8]], A.is_ge, 0.0, 15, -1, ["bo"], ["bo"])
    num(T.k77[:, 0:4], [[77, 4]], -77, 0, "k77")
    sel(T.idf[:, :], T.one[:, :], [[-1, 128]], A.is_equal, 0.0, 0, 1, ["one"], ["idf"])

    def spread(m, src, r0):
        o = T.sp[0:25, m * 128:m * 128 + 128]
        sel(o, src[0:25, :], [[1, 128]], A.is_ge, 0.0, 16 * r0, -16, ["one", "k613"], [("sp", m)])
        sel(o, o, [[-1, 128]], A.is_ge, 0.0, 15 - 16 * r0, 16, [("sp", m)], [("sp", m)])

    spread(0, T.one, 0)
    send_start(0)
    sel(T.lu[0:25, :], T.sp[0:25, 0:128], [[0, 128]], A.is_gt, 64.0, 24, -1, [("sp", 0)], ["lu"])
    num(T.k613[0:25, :], [[0, 8], [613, 16]], 0, 0, "k613")
    spread(2, T.one, 16)
    spread(3, T.k613, 8)

    def kappa_rows():
        tsc(T.kl[:, 0:4], T.k77[:, 0:4], T.kc[:, 0:1], A.add, ["k77", "kc"], ["kl"])

    def constants_b():
        tsc(T.wia[:, 0:1], T.wti[:, :], 0xF00, A.bitwise_and, ["wti"], ["wia"])
        tsc(T.wia[:, 1:2], T.wti[:, :], 255, A.bitwise_and, ["wti"], ["wib"])
        tcopy(T.rb1[:, 0:8], T.bo[:, :], ["bo"], ["rb1"])
        tcopy(T.wf[:, 0:2], T.wia[:, 0:2], ["wia", "wib"], ["wf"])
        tsc(T.rb3[:, 0:8], T.bo[:, :], -1.0, A.mult, ["bo"], ["rb3"])
        tsc(T.rb1[:, 8:16], T.bo[:, :], T.wf[:, 0:1], A.mult, ["bo", "wf"], ["rb1b"])
        tsc(T.rb2[:, 8:16], T.bo[:, :], T.wf[:, 1:2], A.mult, ["bo", "wf"], ["rb2b"])
        kappa_rows()
        tsc(T.lp[0:25, :], T.sp[0:25, 0:128], 2048.0, A.mult, [("sp", 0)], ["lp"])
        for m in (2, 3):
            o = T.sx[0:25, (m - 2) * 128:(m - 1) * 128]
            tsc(o, T.sp[0:25, m * 128:m * 128 + 128], 64.0, A.mult, [("sp", m)], [("sx", m)])
            ttens(T.lp[0:25, :], T.lp[0:25, :], o, A.add, [("sx", m), "lp"], ["lp"])
        sel(T.lp[0:25, :], T.lp[0:25, :], [[0, 128]], A.is_gt, float(2048 * 64 + 64 * 77 - (1 << 23)), 24, -1, ["lp"], ["lp"])
        for h in range(2):
            sel(T.per[0:96, h * 48:h * 48 + 48], T.oneb[0:96, 0:48], [[8, 3], [24, 4], [2, 4]], A.is_equal, 0.0, h, -1,
                ["oneb"], [("per", h)])
        num(T.c16[:, :], [[0, 16], [16, 4]], 16, 0, "c16")
        num(T.ian[:, :], [[0, 16]], 0, 1, "ian")
        num(T.iav[:, :], [[16, 16]], 0, 0, "iav")
        num(T.tmi[:, :], [[-1, 256]], 4096, 1, "tmi")
        spread(1, T.one, 8)

    def constants_c():
        tcopy(T.slb[0:96, :], T.sli[0:96, :], ["sli"], ["slb"])
        for t in range(RO):
            for h in range(2):
                for i in range(2):
                    o = t * 64 + h * 32 + i * 16
                    mm(T.ps7[:, o:o + 16], T.slb[0:96, i * 128:i * 128 + 128], T.per[0:96, h * 48 + t * 16:h * 48 + t * 16 + 16],
                       True, True, ["slb", ("per", h)], ["ps7"])
        tcopy(T.idb[:, :], T.idf[:, :], ["idf"], ["idb"])
        tsc(T.tmi[:, :], T.tmi[:, :], 15, A.bitwise_and, ["tmi"], ["tmi"])
        tsc(T.ian[:, :], T.ian[:, :], 15, A.bitwise_and, ["ian"], ["ian"])
        tsc(T.diag[:, :], T.tmi[:, :], 0.0, A.is_equal, ["tmi"], ["diag"], 16.0, A.mult)
        ttens(T.ian[:, :], T.ian[:, :], T.iav[:, :], A.add, ["ian", "iav"], ["ian"])
        for h in range(2):
            tcopy(T.r8[0:16, h * 128:h * 128 + 128], T.sp[0:16, h * 128:h * 128 + 128], [("sp", h)], [("r8", h)])
        tsc(T.iav[:, :], T.ian[:, :], 16.0, A.mult, ["ian"], ["iav"])
        tcopy(T.a4[:, :], T.ps7[:, 0:192], ["ps7"], ["a4"])

    def start_names(t):
        both = [("L", t, 0, 0), ("L", t, 0, 1)]
        if t:
            tcopy(T.nm[:, 0:256], T.lst[:, lists(t, 0)], both, [("nm", 0, 0), ("nm", 0, 1)])
        tsc(T.nc[:, :], T.lst[:, lists(t, 0)], -2048.0, A.add, both, [("nc", 0), ("nc", 1)])

    slot, mslot, where = [0], [0], {}

    def gather(q, key, src, a, reads, p0, p1):
        if key not in where:
            slot[0] = (slot[0] + 1) % NG
            where[key] = slot[0]
        s = where[key]
        out = T.gat[:, s * SEG + p0 * N:s * SEG + p1 * N]
        win = T.tab[:, :].indirect(src[:, a + p0 * 32:a + p1 * 32])
        keys = [("g", s, p) for p in range(p0, p1)]
        if q == "s":
            run("s", reads + ["tab"], keys, lambda e: e.activation(out, win, COPY))
        else:
            V(reads + ["tab"], keys, lambda e: e.tensor_copy(out, win))

    def gather_own(q, t, l, h, p0=0, p1=4):
        gather(q, ("o", t, l, h), T.lst, (t * 5 + l) * 256 + h * 128, [("L", t, l, h)], p0, p1)

    def shared(l, h):
        return h == 1 and l < 4

    def gather_client(q, t, l, h, p0=0, p1=4):
        if q == "s" and shared(l, h):
            p1 = 3
        gather(q, ("c", t, l, h), T.clst, (t * 5 + l) * 256 + h * 128, [("cl", t, 0) if l == 0 else ("cl", t, l, h)], p0, p1)

    def scans(key):
        s = where[key]
        kind, t, l, h = key
        m = mslot[0] = mslot[0] ^ 1
        buf, y0, yk = (T.ymax, l * 4096 + h * SEG, ("y", l, h)) if kind == "o" else (T.cmax, h * SEG, ("cy", h))
        if kind == "c" and shared(l, h):
            gather_client("v", t, l, h, 3, 4)
            yield
        for p in range(NP):
            x = T.gat[:, s * SEG + p * N:s * SEG + p * N + N]
            scan(buf[:, y0 + p * N:y0 + p * N + N], T.mkx[:, :], x, 0.0, A.min, A.max, ["mkx", ("g", s, p)], [yk + (p,)])
            yield
        for p in range(NP):
            x = T.gat[:, s * SEG + p * N:s * SEG + p * N + N]
            scan(T.ymin[:, m * SEG + p * N:m * SEG + p * N + N], T.mkn[:, :], x, 255.0, A.max, A.min, ["mkn", ("g", s, p)], [("m", m, p)])
            if p < NP - 1:
                yield
        y, mn = buf[:, y0 + 15:y0 + SEG:16], T.ymin[:, m * SEG + 15:(m + 1) * SEG:16]
        YP, MP = [yk + (p,) for p in range(NP)], [("m", m, p) for p in range(NP)]
        if kind == "o":
            b = "ps%d" % h
            out = T[b][:, 0:16]
            mm(out, y, T.rb1[:, :], True, False, ["rb1", "rb1b"] + YP, [b])
            mm(out, y, T.rb2[:, :], False, False, ["rb2", "rb2b"] + YP, [b])
            mm(out, mn, T.rb3[:, :], False, True, ["rb3", "rb3b"] + MP, [b])
        else:
            out = T.ps2[:, h * 8:h * 8 + 8]
            mm(out, y, T.rb1[:, 0:8], True, False, ["rb1"] + YP, ["ps2"])
            mm(out, mn, T.rb3[:, 0:8], False, True, ["rb3"] + MP, ["ps2"])
        yield

    def stream(*keys):
        for key in keys:
            for _ in scans(key):
                yield

    def drive(chain, filler):
        for k in chain:
            for _ in range(k):
                next(filler, None)

    def drain(filler):
        for _ in filler:
            pass

    def keep_spans(t, l):
        a = t * 80
        o = T.eret[:, a + l:a + 64:4] if l < 4 else T.eret[:, a + 64:a + 80]
        tcopy(o, T.ps2[:, 0:16], ["ps2"], [("er", t, l)])

    def return_spans(t, part):
        a = t * 80 + (64 if part else 0)
        n = 16 if part else 64
        ls = [4] if part else range(4)
        send(client[t], T.eqin[:, a:a + n], T.eret[:, a:a + n], "e%d_%d" % (part + 1, t), [("er", t, l) for l in ls])

    def step(t, l, h, keep):
        c = slice(h * 128, h * 128 + 128)
        b = "ps%d" % h
        E, U = T[b][:, 0:8], T[b][:, 8:16]
        es, hd = T.es[:, h * 8:h * 8 + 8], T.hd[:, h * 8:h * 8 + 8]
        um = T.um[:, h * 8:h * 8 + 8]
        o = (l * 2 + h) * 24
        H = T.tt[:, o + 8:o + 16]
        j = l - 1
        yield 2
        if l:
            D = T.darr[:, h * 32 + j:h * 32 + 32:4]
            Ua = T.uarr[:, h * 32 + j:h * 32 + 32:4]
            a = T.a4[:, t * 64 + h * 32 + j:t * 64 + h * 32 + 32:4]
            ttens(D, E, es, A.subtract, [b, ("es", h), "D"], [("D", j, h)])
            tcopy(Ua, U, [b, "U"], [("U", j, h)])
            yield 1
            if l == 4:
                ttens(T.h3[:, h * 8:h * 8 + 8], D, a, A.is_le, [("D", j, h), "a4"], [("h3", h)])
                return
            ttens(H, D, a, A.is_le, [("D", j, h), "a4"], [("th", l, h)])
            tsc(um, Ua, 4095, A.bitwise_and, [("U", j, h)], [("um", h)])
            yield 1
            tsc(T.tt[:, o + 16:o + 24], H, T.kl[:, l:l + 1], A.mult, [("th", l, h), "kl"], [("tk", l, h)])
            ttens(T.tt[:, o:o + 8], um, H, A.mult, [("um", h), ("th", l, h)], [("tu", l, h)])
        else:
            u0 = T.u0[:, h * 8:h * 8 + 8]
            tcopy(u0, U, [b], [("u0", h)])
            fill(H, 1.0, [("th", 0, h)])
            tcopy(es, E, [b], [("es", h)])
            yield 1
            tsc(um, u0, 4095, A.bitwise_and, [("u0", h)], [("um", h)])
            tsc(T.tt[:, o + 16:o + 24], H, T.kl[:, 0:1], A.mult, [("th", l, h), "kl"], [("tk", l, h)])
            yield 1
            tcopy(T.tt[:, o:o + 8], um, [("um", h)], [("tu", 0, h)])
        mm(T.ps4[0:24, c], T.tt[:, o:o + 24], T.idf[:, :], True, True, [("tu", l, h), ("th", l, h), ("tk", l, h), "idf"], ["ps4"])
        if l:
            ttens(hd, H, D, A.mult, [("th", l, h), ("D", j, h)], [("hd", h)])
        yield 3
        r = T.row[0:25, c]
        tcopy(T.row[0:24, c], T.ps4[0:24, c], ["ps4"], [("row", h)])
        mm(T.ps5[:, 0:128], T.lu[0:25, :], r, True, True, ["lu", ("row", h)], ["ps5"])
        mm(T.ps6[:, 0:128], T.lp[0:25, :], r, True, True, ["lp", ("row", h)], ["ps6"])
        if l:
            ttens(es, es, hd, A.add, [("es", h), ("hd", h)], [("es", h)])
        yield 3
        n = T.nm[:, (l + 1) * 256 + h * 128:(l + 1) * 256 + h * 128 + 128]
        L = T.lst[:, lists(t, l + 1, h)]
        ttens(T.pt[:, c], T.ps5[:, 0:128], T.nc[:, c], A.mult, ["ps5", ("nc", h)], [("pt", h)])
        yield 1
        ttens(T.qt[:, c], T.ps6[:, 0:128], T.pt[:, c], A.add, ["ps6", ("pt", h)], [("qt", h)])
        if keep:
            keep_spans(t, l - 1)
        yield 1
        tsc(n, T.qt[:, c], 6, A.arith_shift_right, [("qt", h)], [("nm", l + 1, h)], 4095, A.bitwise_and)
        yield 1
        tcopy(L, n, [("nm", l + 1, h)], [("L", t, l + 1, h)])
        send(partner[t], T.clst[:, lists(t, l + 1, h)], L, "r%d_%d_%d" % (t, l + 1, h), [("L", t, l + 1, h)])
        if l < 3:
            tsc(T.nc[:, c], n, -2048.0, A.add, [("nm", l + 1, h)], [("nc", h)])

    def copy_guesses():
        for l in range(1, 4):
            for h in range(2):
                o = (l * 2 + h) * 24
                i = T.tt[:, o + 8:o + 16]
                d = T.h1[:, h * 32 + l:h * 32 + 32:4]
                run("s", [("th", l, h)], [("h1x", l, h)], lambda e, i=i, d=d: e.activation(d, i, COPY))

    def settle(t):
        b = t * 80
        HK = [("h1", 0)] + [("h1x", l, h) for l in range(1, 4) for h in range(2)]
        DK = [("D", j, h) for j in range(4) for h in range(2)]
        UK = [("U", j, h) for j in range(4) for h in range(2)]
        e1 = ("e1", t)
        m63 = slice(0, 63)
        a = t * 64
        tsc(T.nh[:, :], T.h1[:, :], -1.0, A.mult, HK, ["nh"], 1.0, A.add)
        tsc(T.lowa[:, :], T.uarr[:, :], 15, A.bitwise_and, UK + ["U"], ["lowa"])
        tsc(T.low0[:, :], T.u0[:, :], 15, A.bitwise_and, [("u0", 0), ("u0", 1)], ["low0"])
        yield 1
        ttens(T.cod[:, :], T.lowa[:, :], T.c16[:, :], A.add, ["lowa", "c16"], ["cod"])
        yield 1
        ttens(T.he[:, :], T.h1[:, :], T.eqin[:, b:b + 64], A.mult, HK + [e1], ["he"])
        yield 1
        keep_spans(t, 4)
        return_spans(t, 1)
        scan(T.esq[:, :], T.nh[:, :], T.he[:, :], 0.0, A.mult, A.add, ["nh", "he"], ["esq"])
        yield 1
        ttens(T.dq[:, m63], T.eqin[:, b + 1:b + 64], T.esq[:, m63], A.subtract, [e1, "esq"], ["dq"])
        yield 1
        ttens(T.dtt[:, m63], T.dq[:, m63], T.darr[:, m63], A.add, ["dq", "D"] + DK, ["dtt"])
        yield 1
        ttens(T.dd[:, m63], T.dtt[:, m63], T.a4[:, a:a + 63], A.is_le, ["dtt", "a4"], ["dd"])
        yield 1
        ttens(T.ne[:, 1:64], T.dd[:, m63], T.h1[:, 1:64], A.not_equal, ["dd", "ne0"] + HK, ["ne"])
        yield 2
        scan(T.wre[:, :], T.ne[:, 0:64], T.mk[:, :], 0.0, A.max, A.mult, ["ne", "ne0", "mk"], ["wre"])
        for _ in step(t, 4, 1, False):
            pass
        ttens(T.go[:, m63], T.dd[:, m63], T.wre[:, m63], A.is_gt, ["dd", "wre"], ["go"])
        tsc(T.nw[:, :], T.wre[:, 3::4], -1.0, A.mult, ["wre"], ["nw"], 1.0, A.add)
        tsc(T.low4[:, :], T.uarr[:, 3::4], 15, A.bitwise_and, [("U", 3, 0), ("U", 3, 1)], ["low4"])
        ttens(T.gco[:, m63], T.go[:, m63], T.cod[:, m63], A.mult, ["go", "cod"], ["gco"])
        ttens(T.th0[:, :], T.a4[:, a + 3:a + 64:4], T.darr[:, 3::4], A.subtract, ["a4", ("D", 3, 0), ("D", 3, 1)], ["th0"])
        tsc(T.cod4[:, :], T.low4[:, :], 64.0, A.add, ["low4"], ["cod4"])
        scan(T.sco[:, m63], T.mk[:, m63], T.gco[:, m63], 0.0, A.mult, A.max, ["mk", "gco"], ["sco"])
        ttens(T.thr[:, :], T.th0[:, :], T.esq[:, 3::4], A.add, ["th0", "esq"], ["thr"])
        ttens(T.c4m[:, :], T.cod4[:, :], T.nw[:, :], A.mult, ["cod4", "nw"], ["c4m"])
        ttens(T.cp[:, :], T.sco[:, 2:63:4], T.low0[:, :], A.max, ["sco", "low0"], ["cp"])

    def finish(t):
        b = t * 80 + 64
        last = t == RO - 1
        ttens(T.d3[:, :], T.eqin[:, b:b + 16], T.thr[:, :], A.is_le, [("e2", t), "thr"], ["d3"])
        ttens(T.gcx[:, :], T.d3[:, :], T.c4m[:, :], A.mult, ["d3", "c4m"], ["gcx"])
        ttens(T.cd[:, :], T.gcx[:, :], T.cp[:, :], A.max, ["gcx", "cp"], ["cd"])
        mm(T.ps4[0:16, 0:128], T.cd[:, :], T.idb[:, :], True, True, ["cd", "idb"], ["ps4"])
        if not last:
            ttens(T.ne3[:, :], T.d3[:, :], T.h3[:, :], A.not_equal, ["d3", ("h3", 0), ("h3", 1)], ["ne3"])
        tcopy(T.rc[0:16, :], T.ps4[0:16, 0:128], ["ps4"], ["rc"])
        for h in range(2):
            mm(T.ps5[:, h * 128:h * 128 + 128], T.r8[0:16, h * 128:h * 128 + 128], T.rc[0:16, :], True, True, [("r8", h), "rc"], ["ps5"])
        if not last:
            ttens(T.wr[:, :], T.ne3[:, :], T.wre[:, 3::4], A.max, ["ne3", "wre"], ["wr"])
            mm(T.ps7[:, 0:16], T.oneb[:, :], T.wr[:, :], True, True, ["oneb", "wr"], ["ps7"])
        ttens(T.cm[:, :], T.ps5[:, 0:256], T.diag[:, :], A.mult, ["ps5", "diag"], ["cm"])
        scan(T.lsc[:, :], T.mkl[:, :], T.cm[:, :], 0.0, A.mult, A.max, ["mkl", "cm"], ["lsc"])
        ci = T.lsc[:, 15::16]
        tsc(T.ca[:, :], ci, 0x700, A.bitwise_and, ["lsc"], ["ca"])
        tsc(T.lo[:, :], ci, 4, A.arith_shift_right, ["lsc"], ["lo"], 15, A.bitwise_and)
        ttens(T.off[:, :], T.ca[:, :], T.ian[:, :], A.add, ["ca", "ian"], ["off"])
        ttens(T.vi[:, :], T.lo[:, :], T.iav[:, :], A.add, ["lo", "iav"], ["vi"])
        tsc(T.yl[:, :], T.off[:, :], 16.0, A.mult, ["off"], ["yl"], 15.0, A.add)
        YK = [("y", l, h, p) for l in range(5) for h in range(2) for p in range(NP)]
        run("s", YK + ["yl"], ["fy"], lambda e: e.activation(T.fy[:, :], T.ymax[:, :].indirect(T.yl[:, :]), COPY))
        tcopy(T.nl[:, :], T.off[:, :], ["off"], ["nl"])
        tcopy(T.vu[:, :], T.vi[:, :], ["vi"], ["vu"])
        NK = [("nm", l, h) for l in range(5) for h in range(2)]
        win = T.nm[:, :].indirect(T.nl[:, :])
        if last:
            tsc(T.vu[:, 8:16], T.vi[:, 8:16], -2048.0, A.add, ["vi", "vu"], ["vub"])
            for h, q in ((0, "s"), (1, "y")):
                c = slice(h * 128, h * 128 + 128)
                half = T.tab[:, h * 2048:h * 2048 + 2048]
                vl = half.indirect(T.vu[:, h * 8:h * 8 + 8])
                ttens(T.sm[:, c], vl, T.fy[:, c], A.add, ["tab", "vu", "vub", "fy"], [("sm", h)])
                tsc(T.sh[:, c], T.sm[:, c], 1, A.arith_shift_right, [("sm", h)], [("sh", h)])
                V([("sh", h), "vu", "vub", "tab"], [("tabh", h)], lambda e, vl=vl, c=c: e.tensor_copy(vl, T.sh[:, c]))
                run(q, [("tabh", h)], [], lambda e, h=h, half=half: e.dma_start(T.yx[:, h * 2048:h * 2048 + 2048], half), "stx%d" % h, 16)
            tcopy(T.ycf[:, :], win, NK + ["nl"], ["ycf"])
            run("y", ["ycf"], [], lambda e: e.dma_start(T.yc[:, :], T.ycf[:, :]), "stc", 16)
        else:
            tcopy(T.lst[:, lists(t + 1, 0)], win, NK + ["nl"], [("L", t + 1, 0, 0), ("L", t + 1, 0, 1)])
            send_start(t + 1)
            ttens(T.sm[:, :], T.tab[:, :].indirect(T.vu[:, :]), T.fy[:, :], A.add, ["tab", "vu", "fy"], [("sm", 0), ("sm", 1)])
            tsc(T.sh[:, :], T.sm[:, :], 1, A.arith_shift_right, [("sm", 0)], [("sh", 0), ("sh", 1)])
            V([("sh", 0), "vu"], ["tab"], lambda e: e.tensor_copy(T.tab[:, :].indirect(T.vu[:, :]), T.sh[:, :]))

    def new_kappa():
        V(["ps7"], ["ki0"], lambda e: e.tensor_reduce(T.kc[:, 1:2], T.ps7[:, 0:16], AxisListType.X, A.add))
        yield 1
        tcopy(T.ki[:, 0:1], T.kc[:, 1:2], ["ki0"], ["ki1"])
        yield 1
        tsc(T.ki[:, 1:2], T.ki[:, 0:1], 31, A.bitwise_and, ["ki1"], ["ki2"])
        yield 1
        tcopy(T.kc[:, 0:1], T.ki[:, 1:2], ["ki2"], ["kc"])
        yield 1
        kappa_rows()

    for t in range(RO):
        O = lambda l, h: ("o", t, l, h)
        K = lambda l, h: ("c", t, l, h)
        gather_own("s", t, 0, 0, 0, 2)
        gather_own("v", t, 0, 0, 2, 4)
        gather_own("s", t, 0, 1)
        gather_client("s", t, 0, 0)
        first = stream(O(0, 0))
        if t:
            drive(new_kappa(), first)
        start_names(t)
        if t == 0:
            constants_b()
        drain(first)
        for l in range(4):
            f = stream(*([K(l - 1, 1)] if l else []), O(l, 1))
            drive(step(t, l, 0, l > 0), f)
            gather_own("s", t, l + 1, 0)
            gather_client("s", t, l, 1)
            drain(f)
            if l == 0 and t == 0:
                constants_c()
            f = stream(K(l, 0), O(l + 1, 0))
            drive(step(t, l, 1, False), f)
            if l < 3:
                gather_own("s", t, l + 1, 1)
            gather_client("s", t, l + 1, 0)
            drain(f)
        gather_client("s", t, 4, 1)
        copy_guesses()
        gather_own("s", t, 4, 1, 0, 2)
        f = stream(K(3, 1), K(4, 0))
        drive(step(t, 4, 0, False), f)
        for _ in range(2 * NP):
            next(f)
        keep_spans(t, 3)
        return_spans(t, 0)
        gather_own("v", t, 4, 1, 2, 4)
        drain(f)
        drain(stream(K(4, 1)))
        f = stream(O(4, 1))
        drive(settle(t), f)
        drain(f)
        finish(t)
    for s in sorted(total):
        need("g", s, total[s])
